import numpy as np, ml_dtypes
CORES = [3,11,19,27,35,43,51,59]
N = 8
import mx_ref
BF = ml_dtypes.bfloat16
def entries(a):
    return np.ascontiguousarray(a.T).reshape(-1)
def table(e):
    return np.ascontiguousarray(np.reshape(e, (-1, 16)).T).astype(np.int32)
def pick(q, e):
    c = np.concatenate([q[0].reshape(128, -1, 4), np.zeros((128, 1, 4), np.uint8)], axis=1); s = np.concatenate([q[1], np.ones((16, 1), np.uint8)], axis=1)
    return (np.ascontiguousarray(c[:, e].reshape(128, -1)), np.ascontiguousarray(s[:, e]))
def join(*qs):
    return (np.concatenate([q[0] for q in qs], axis=1), np.concatenate([q[1] for q in qs], axis=1))
def put(q, e, v):
    c, s = q[0].reshape(128, -1, 4).copy(), q[1].copy(); c[:, e] = v[0].reshape(128, -1, 4); s[:, e] = v[1]
    return (c.reshape(128, -1), s)
def pk(c, s):
    return (np.ascontiguousarray(c), mx_ref.live(s))
def emit(q):
    return q[0], q[1]
def decode(q):
    o = []
    for b in range(4):
        e = np.zeros((128, 128, 4), np.float32); e[np.arange(128), np.arange(128), b] = 1
        o.append(mx_ref.matmul(mx_ref.quantize(e.reshape(128, 512).astype(BF)), q))
    return np.stack(o, axis=2).reshape(128, -1)
def cut(t, i, w=512):
    return t[:, w * i:w * i + w]
def f(rng, *shape):
    return mx_ref.flush((rng.standard_normal(shape, dtype=np.float32) * np.exp2(rng.integers(-2, 3, shape[:-1] + (1,)))).astype(BF))
def wide(rng, *shape, cols=0):
    v = rng.standard_normal(shape, dtype=np.float32) * np.exp2(rng.integers(-12, 13, shape)).astype(np.float32)
    if cols: v *= np.repeat(np.exp2(rng.integers(-cols, cols + 1, shape[:-2] + (1, shape[-1] // 4))) * (rng.random(shape[:-2] + (1, shape[-1] // 4)) > 0.0625), 4, axis=-1).astype(np.float32)
    return mx_ref.flush(v.astype(BF))
P, M, A, CAPP, R = 512, 128, 32, 16, 3
def big(v):
    v = v.astype(np.float32)
    v[np.abs(v) < np.float32(2.0 ** -16)] = 0
    return v.astype(BF)
def listed(e):
    return np.stack([table(v) for v in e])
def setup_inputs(rng):
    return {"ky": big(f(rng, N, 128, 4 * P)), "nx": listed(rng.integers(0, N * M, (N, P))), "x": big(f(rng, N, 128, 4 * A)), "st": listed(rng.integers(0, N * M, (N, A))), "w": f(rng, N, 128, 512)}
def setup_inputs_spread(rng):
    d = setup_inputs(rng)
    d["ky"] = big(wide(rng, N, 128, 4 * P, cols=6))
    d["x"] = big(wide(rng, N, 128, 4 * A, cols=4))
    return d
def setup_inputs_ties(rng):
    d = setup_inputs(rng)
    o = np.argsort(rng.random((N, M, 4)), axis=2) % 2
    v = d["ky"].reshape(N, 128, M, 4, 4)
    v = np.ascontiguousarray(np.stack([np.take_along_axis(v[r], np.broadcast_to(o[r][None, :, :, None], (128, M, 4, 4)), axis=2) for r in range(N)]))
    for r in range(N): v[r][:, rng.permutation(M)[:M // 8]] = 0
    d["ky"] = v.reshape(N, 128, 4 * P)
    to = np.argsort(rng.random((N, M, N)), axis=2)[:, :, :4]
    d["nx"] = listed((to * M + rng.integers(0, M, (N, M, 4))).reshape(N, P))
    return d
def setup_inputs_crowd(rng):
    d = setup_inputs(rng)
    o, st = rng.permutation(N), np.zeros((N, A), int)
    for i in range(N):
        s, to = o[i], o[(i + 1) % N]
        here = rng.permutation(A) < (CAPP if i % 2 == 0 else A - CAPP // 4)
        near = to * M + (rng.integers(0, M, A) if i % 2 == 0 else np.full(A, int(rng.integers(0, M))))
        far = (to + rng.integers(1, N, A)) % N * M + rng.integers(0, M, A)
        st[s] = np.where(here, near, far)
    d["st"] = listed(st)
    return d
def kept(rng, *shape):
    return 4 * rng.integers(0, M // 4, shape) + rng.integers(0, 3, shape)
def setup_inputs_stay(rng):
    d = setup_inputs(rng)
    o = rng.permutation(N)
    z, z2 = int(o[0]), int(o[1])
    v = np.arange(M)[None, :, None]
    to = np.arange(N)[:, None, None] * M + np.where(v % 2 == 0, v, kept(rng, N, M, 4))
    to[z, 3::4] = o[rng.integers(2, N, (M // 4, 4))] * M + rng.integers(0, M, (M // 4, 4))
    to[z2] = z * M + kept(rng, M, 4)
    d["nx"] = listed(to.reshape(N, P))
    leave = np.zeros((N, A), bool)
    leave[:, :CAPP] = np.argsort(rng.random((N, CAPP)), axis=1) < CAPP // 4
    st = z * M + np.where(leave, 4 * rng.integers(0, M // 4, (N, A)) + 3, kept(rng, N, A))
    n = CAPP + CAPP // 2
    st[:, n:] = z2 * M + rng.integers(0, M, (N, A - n))
    low = rng.permutation(N) < N // 2
    st[low] = np.roll(st[low], A - n, axis=1)
    d["st"] = listed(st)
    return d
def setup_inputs_turn(rng):
    d = setup_inputs(rng)
    sign = rng.choice([-1.0, 1.0], (128, 4))
    top = np.arange(128) < 64
    o = np.argsort(rng.random((N, M, 4)), axis=2).reshape(N, P)
    g = np.where(top[None, :, None], np.exp2(-2.0 * o)[:, None, :], np.exp2(2.0 * o + 2)[:, None, :])
    d["ky"] = big(((1 + rng.random((N, 128, P, 4))) * g[..., None] * sign[None, :, None, :]).reshape(N, 128, 4 * P))
    d["x"] = big(((1 + rng.random((N, 128, A, 4))) * top[None, :, None, None] * sign[None, :, None, :]).reshape(N, 128, 4 * A))
    return d
def check_inputs(d):
    b = []
    for k, lo, hi in (("ky", -16, 24), ("x", -16, 24), ("w", -30, 30)):
        v = np.abs(d[k].astype(np.float32))
        if not (np.isfinite(v).all() and ((v == 0) | (v >= 2.0 ** lo) & (v <= 2.0 ** hi)).all()): b.append("a value of " + k)
    for k in ("nx", "st"):
        if d[k].min() < 0 or d[k].max() >= N * M: b.append("an entry of " + k)
    return b
def served(node):
    ok = np.zeros(N * A, bool)
    for s in range(N):
        at = node[A * s:A * s + A] // M
        for d in range(N): ok[A * s + np.flatnonzero(at == d)[:CAPP]] = True
    return np.flatnonzero(ok)
def reference(ky, nx, x, st, w):
    pieces = [mx_ref.quantize(np.ascontiguousarray(cut(ky[d], i))) for d in range(N) for i in range(P // 128)]
    dk = decode(join(*pieces)).reshape(128, N * P, 4)
    leads = np.concatenate([entries(nx[d]) for d in range(N)])
    q = join(*[mx_ref.quantize(np.ascontiguousarray(x[s])) for s in range(N)])
    node = np.concatenate([entries(st[s]) for s in range(N)])
    e = np.arange(N * A)
    way = [node]
    for t in range(R):
        go = served(node)
        z = np.concatenate([mx_ref.matmul(p, q) for p in pieces])
        four = 4 * node[:, None] + np.arange(4)
        k = 4 * node + np.argmax(z[four, e[:, None]] + np.float32(0), axis=1)
        v = decode(q).reshape(128, N * A, 4) * np.float32(0.5) + dk[:, k] * np.float32(0.5)
        new = mx_ref.quantize(np.ascontiguousarray(v.reshape(128, -1).astype(BF)))
        q = put(q, go, pick(new, go))
        node = node.copy()
        node[go] = leads[k[go]]
        way.append(node)
    oc, osc = np.zeros((N, 128, 4 * A), np.uint8), np.zeros((N, 16, A), np.uint8)
    nd, y = np.zeros((N, R + 1, A), np.float32), np.zeros((N, 128, A), np.float32)
    for s in range(N):
        own = pick(q, np.arange(A * s, A * s + A))
        oc[s], osc[s] = emit(own)
        nd[s] = np.stack(way)[:, A * s:A * s + A]
        y[s] = mx_ref.matmul(mx_ref.quantize(np.ascontiguousarray(w[s])), own)
    return {"oc": oc, "osc": osc, "nd": nd, "y": y}

@@ -1,0 +1,634 @@
+from concourse.bass import DstId, RemoteDMATransfer
+from concourse.mybir import dt, AluOpType, AxisListType, ActivationFunctionType
+
+R, A, P, CAP, N = 3, 32, 512, 16, 8
+HOME = A + N * CAP
+FIRST, REST = (1, 2), (3,)
+OWN, KEPT, STEP = 12, 13, 14
+RANK = 32768
+TURN, GATE = 2 ** 18, 2 ** 24
+FLOOR = 2.0 ** -17 - 0.5
+HELPERS = 2
+XKEEP = 4
+KEEP = 1
+HALF = N * CAP // HELPERS
+HAND = 4
+LEGS = ["x", "b0", "f1", "b1", "f2", "b2"]
+
+SCRATCH = {}
+
+
+def _sb(name, cols, ty):
+    SCRATCH[name] = ("sbuf", [128, cols], ty)
+
+
+_F, _I, _U, _B, _Q, _S = "float32", "int32", "uint16", "bfloat16", "float8_e4m3fn_x4", "uint8"
+for _n, _c, _t in [
+    ("eF", 516, _B), ("iw", 128, _B), ("ia", 32, _I), ("ia2", 32, _I), ("ic", 32, _I), ("ic2", 32, _I), ("mask", 64, _F),
+    ("ip", 1, _I), ("ip15", 1, _I), ("ip5", 1, _I), ("ip31", 1, _I), ("ip3", 1, _I), ("ipf", 1, _F),
+    ("r1", 1, _F), ("k0", 1, _F), ("tb", 1, _F), ("af", 1, _F), ("t4", 1, _F), ("cl1", 1, _F), ("r4", 1, _F),
+    ("cloc", 1, _F), ("i8", 8, _I), ("i82", 8, _I), ("mask8", 8, _F), ("ja", 64, _F), ("rowb", 64, _F), ("rowx", 64, _F), ("ct", 64, _F),
+    ("rst", 64, _F), ("one", 73, _F), ("c1s", 4, _F), ("ik", 32, _I),
+    ("ku", 32, _U), ("stt", 3, _I), ("nxa", 32, _I), ("nxf", 32, _F), ("nxt", 32, _F),
+    ("nrow", 512, _F), ("tab", 512, _F), ("xb", 512, _B), ("kb", 2048, _B), ("wb", 512, _B), ("yb", 32, _F), ("m0", 128, _B), ("m1", 128, _B),
+    ("kd", 2048, _F),
+]:
+    _sb(_n, _c, _t)
+for _n, _c in [("kn", 512), ("kj", 512), ("wq", 128), ("e0", 128), ("e1", 128), ("e2", 128), ("e3", 128), ("hq0", 128), ("fin", 128), ("la", N * A)]:
+    _sb(_n + "c", _c, _Q)
+    _sb(_n + "s", _c, _S)
+for _t in range(R):
+    for _n, _c in [("sd", 128), ("ld", 128), ("qn", 128)]:
+        if _n != "sd" or _t > 0:
+            _sb("%s%dc" % (_n, _t), _c, _Q)
+            _sb("%s%ds" % (_n, _t), _c, _S)
+    _sb("hq%dc" % (_t + 1), HOME, _Q)
+    _sb("hq%ds" % (_t + 1), HOME, _S)
+    _sb("pk%d" % _t, 8, _I)
+    _sb("vl%d" % _t, 12, _I)
+    _sb("sn%d" % _t, 32, _F)
+    _sb("nl%d" % (_t + 1), 80, _F)
+    _sb("dq%d" % _t, 512, _F)
+    _sb("hb%d" % _t, 512, _B)
+_sb("hxc", A, _Q)
+for _l in LEGS:
+    _sb("h%ss" % _l, A if _l == "x" else HALF, _S)
+SMALL, WIDE = {}, {"f": ["smf", 0], "i": ["smi", 0], "u": ["smu", 0]}
+
+
+def _small(ty, name, cols):
+    w = WIDE[ty]
+    SMALL[name] = (w[0], w[1], w[1] + cols)
+    w[1] += cols + cols % 2
+
+
+for _t in range(R + 1):
+    for _n, _c in [("u", 1), ("bc", 73), ("bt", 64), ("pkq", 64), ("ind", 64), ("cum", 64), ("pkr", 64), ("sp", 64),
+                   ("q0", 8), ("n", 1), ("lm", 32), ("lsc", 32), ("vp", 8), ("pkf", 1), ("vf", 1), ("a1", 1),
+                   ("c1", 1), ("i0", 64), ("oh", 64), ("oht", 64), ("q1", 1), ("dp", 1), ("p0", 128), ("p1", 128), ("p2", 128), ("p3", 128),
+                   ("s4", 4), ("mx", 1), ("ne", 4), ("js", 4), ("d0", 64), ("dt", 64), ("ds", 64), ("lf", 32),
+                   ("n1", 32), ("j0", 128), ("j1", 128), ("j2", 128)]:
+        _small("f", "%s_%d" % (_n, _t), _c)
+    for _n, _c in [("li", 32), ("be", 64), ("sr", 8), ("ui", 1), ("ni", 1), ("lr", 32), ("pki", 1), ("vi", 1), ("ai", 1)]:
+        _small("i", "%s_%d" % (_n, _t), _c)
+    for _n, _c in [("su", 8), ("lu", 2), ("ko", 32), ("l2u", 2)]:
+        _small("u", "%s_%d" % (_n, _t), _c)
+_sb("smf", WIDE["f"][1], _F)
+_sb("smi", WIDE["i"][1], _I)
+_sb("smu", WIDE["u"][1], _U)
+for _b in range(4):
+    SCRATCH["z%d" % _b] = ("psum", [128, 512], "float32")
+    SCRATCH["d%d" % _b] = ("psum", [128, 512], "float32")
+
+SEMAPHORES = ["qv", "qs", "qt", "qg", "ls"] + ["m%d" % _k for _k in range(40)] + ["h" + _l for _l in LEGS]
+for _t in range(R):
+    SEMAPHORES += ["apk%d" % _t, "aco%d" % _t, "adl%d" % _t, "are%d" % _t]
+
+
+def helpers_of(core, T, topo):
+    can = [c for c in topo.cores_of(core) if T.rank_of(c) is None and all(topo.may_write(c, r) for r in T.cores)]
+    return sorted(can, key=lambda c: topo.die(c) == topo.die(core))[:HELPERS]
+
+
+def lanes(n, width=8):
+    calls = []
+    while n:
+        k = 1
+        while 2 * k <= min(n, width):
+            k *= 2
+        w = width // k
+        calls.append([tuple(range(w * i, w * i + w)) for i in range(k)])
+        n -= k
+    return calls
+
+
+def parts(leg, s):
+    out = {"c": [], "s": []}
+    if leg == "x":
+        to = [((s + 1 + b) % N, 0) for b in range(N - 1)]
+        cut = XKEEP + (N - XKEEP) // 2
+        out["c"] = [(None, to[:XKEEP], lanes(XKEEP)), (0, to[XKEEP:cut], lanes(cut - XKEEP)), (1, to[cut:], lanes(N - 1 - cut))]
+        m = (N - 1) // 2
+        out["s"] = [(0, to[:m], lanes(m)), (1, to[m:], lanes(N - 1 - m))]
+        return out
+    to = [((s + i) % N, (s + i) % N) for i in range(1, N)]
+    out["c"].append((None, to, [[(i,) for i in range(6)] + [(6, 7)]]))
+    by = [[e for e in to if e[1] * HELPERS // N == h] for h in range(HELPERS)]
+    own = max(by, key=len)[-KEEP:]
+    out["s"].append((None, own, [[(6, 7)]]))
+    for h in range(HELPERS):
+        l = [e for e in by[h] if e not in own]
+        out["s"].append((h, l, lanes(len(l))))
+    return out
+
+
+def landing(leg, s, d):
+    if leg == "x":
+        return "la", A * s, A
+    if leg[0] == "f":
+        return "ld" + leg[1], CAP * s, CAP
+    return "hq%d" % (int(leg[1]) + 1), A + CAP * ((s - d - 1) % N), CAP
+
+
+def sem_of(leg):
+    return "aco0" if leg == "x" else {"f": "aco", "b": "are"}[leg[0]] + leg[1]
+
+
+def issue(g, core, T, topo, leg, s, what, src, first, entries, calls, total):
+    todo = list(entries)
+    for call in calls:
+        tr = []
+        for at in call:
+            d, b = todo.pop(0)
+            dst = T.cores[d]
+            rid, pid, _ = topo.addr(dst)
+            es = topo.engines(core, dst)
+            name, lo, n = landing(leg, s, d)
+            c = CAP * (b - first)
+            o, i = T[name + what][:, lo:lo + n], T[src][:, c:c + n]
+            if what == "c":
+                o, i = o.bitcast(dt.uint8), i.bitcast(dt.uint8)
+            tr.append(RemoteDMATransfer(dst_ids=[DstId(rid=rid, pnc=pid)], dma_engine_mask=sum(1 << es[k] for k in at), remote_sem=T.sem[sem_of(leg)], src=i, dst=o))
+            total["ls"] = total.get("ls", 0) + len(at)
+        g.remote_dma_fused(tr, local_sem=T.sem["ls"])
+
+
+def helper_program(g, core, T, topo):
+    rank = [c for c in topo.cores_of(core) if T.rank_of(c) is not None]
+    if not rank or core not in helpers_of(rank[0], T, topo):
+        return
+    me, s, total = helpers_of(rank[0], T, topo).index(core), T.rank_of(rank[0]), {}
+    for leg in LEGS:
+        g.wait_ge(T.sem["h" + leg], HAND * (2 if leg == "x" else 1))
+        for what, l in parts(leg, s).items():
+            for h, entries, calls in l:
+                if h == me:
+                    issue(g, core, T, topo, leg, s, what, "h" + leg + what, 0 if leg == "x" else N // HELPERS * me, entries, calls, total)
+    g.wait_ge(T.sem["ls"], total["ls"])
+
+
+def rank_program(g, core, T, topo):
+    me = T.rank_of(core)
+    if me is None:
+        helper_program(g, core, T, topo)
+        return
+    OP, X, CP = AluOpType, AxisListType.X, ActivationFunctionType.Copy
+    V, S, TE, Y = g.vector, g.scalar, g.tensor, g.sync
+    eng = {"v": V, "s": S, "t": TE, "g": g, "y": Y}
+    known = {q: {} for q in eng}
+    total, waited = {}, {}
+    wr, rd = {}, {}
+    nm = [0]
+
+    def need(q, evs):
+        for sem, n, clk in sorted(evs, key=lambda e: -sum(e[2].values())):
+            k = known[q]
+            if k.get(sem, 0) < n:
+                eng[q].wait_ge(T.sem[sem], n)
+                k[sem] = n
+                waited[sem] = max(waited.get(sem, 0), n)
+                for x in clk:
+                    k[x] = max(k.get(x, 0), clk[x])
+
+    def before(q, r, w):
+        evs = []
+        for k in r:
+            evs += wr.get(k, [])
+        for k in w:
+            evs += wr.get(k, []) + rd.get(k, [])
+        need(q, evs)
+
+    def done(q, sem, n, r, w, a=()):
+        ev = (sem, n, dict(known[q]))
+        for k in r:
+            rd.setdefault(k, []).append(ev)
+        for k in w:
+            wr[k] = [ev]
+            rd[k] = []
+        for k in a:
+            wr.setdefault(k, []).append(ev)
+
+    def run(q, fn, r=(), w=(), a=()):
+        before(q, r, w)
+        sem = "q" + q
+        fn().then_inc(T.sem[sem], 1)
+        total[sem] = total.get(sem, 0) + 1
+        done(q, sem, total[sem], r, w, a)
+
+    def dma(q, pairs, r=(), w=(), a=()):
+        before(q, r, w)
+        sem = "m%d" % nm[0]
+        nm[0] += 1
+        for o, i in pairs:
+            eng[q].dma_start(o, i).then_inc(T.sem[sem], 16)
+        total[sem] = 16 * len(pairs)
+        done(q, sem, total[sem], r, w, a)
+
+    others = [(me + i) % N for i in range(1, N)]
+    helpers = helpers_of(core, T, topo)
+    NUMBERS = [[(i,) for i in range(6)] + [(6, 7)]]
+    per = lambda plan: sum(len(l) for c in plan for l in c)
+
+    def send(sem, part, r, plan):
+        before("g", r, ())
+        todo = list(others)
+        for call in plan:
+            tr = []
+            for at in call:
+                d = todo.pop(0)
+                dst = T.cores[d]
+                rid, pid, _ = topo.addr(dst)
+                es = topo.engines(core, dst)
+                o, s = part(d)
+                tr.append(RemoteDMATransfer(dst_ids=[DstId(rid=rid, pnc=pid)], dma_engine_mask=sum(1 << es[k] for k in at), remote_sem=T.sem[sem], src=s, dst=o))
+                total["ls"] = total.get("ls", 0) + len(at)
+            g.remote_dma_fused(tr, local_sem=T.sem["ls"])
+
+    def hand(leg, what, src):
+        before("g", (src + what,), ())
+        free = [k for k in topo.engines(core, helpers[0]) if k not in topo.engines(core, T.cores[others[0]])]
+        tr = []
+        for h, c in enumerate(helpers):
+            rid, pid, _ = topo.addr(c)
+            n, lo = (A, 0) if leg == "x" else (HALF, HALF * h)
+            o, i = T["h" + leg + what][:, 0:n], T[src + what][:, lo:lo + n]
+            if what == "c":
+                o, i = o.bitcast(dt.uint8), i.bitcast(dt.uint8)
+            tr.append(RemoteDMATransfer(dst_ids=[DstId(rid=rid, pnc=pid)], dma_engine_mask=sum(1 << k for k in free[HAND * h:HAND * h + HAND]), remote_sem=T.sem["h" + leg], src=i, dst=o))
+            total["ls"] = total.get("ls", 0) + HAND
+        g.remote_dma_fused(tr, local_sem=T.sem["ls"])
+
+    def direct(leg, what, src):
+        before("g", (src + what,), ())
+        for h, entries, calls in parts(leg, me)[what]:
+            if h is None:
+                issue(g, core, T, topo, leg, me, what, src + what, 0, entries, calls, total)
+
+    def coming(leg):
+        n = 0
+        for s in others:
+            for l in parts(leg, s).values():
+                for h, entries, calls in l:
+                    n += sum(len(at) for (d, b), at in zip(entries, [at for call in calls for at in call]) if d == me)
+        return n
+
+    def leave(leg, src):
+        hand(leg, "s", src)
+        direct(leg, "c", src)
+        direct(leg, "s", src)
+
+    def arrive(sem, n, keys):
+        total[sem] = n
+        for k in keys:
+            wr.setdefault(k, []).append((sem, n, {}))
+
+    def ap(name, p=None, c=None):
+        if name in SMALL:
+            buf, lo, hi = SMALL[name]
+            c0, c1, st = (0, hi - lo, 1) if c is None else (c if len(c) == 3 else c + (1,))
+            cols = slice(lo + c0, lo + c1, st)
+        else:
+            buf = name
+            cols = slice(None) if c is None else (slice(*c))
+        rows = slice(None) if p is None else slice(*p)
+        return T[buf][rows, cols]
+
+    def codes(name, lo, hi):
+        return T[name + "c"][:, lo:hi].bitcast(dt.uint8)
+
+    def words(name, lo, hi):
+        return T[name + "c"][:, lo:hi].bitcast(dt.uint32)
+
+    def plane(name, lo, hi):
+        return T[name + "s"][:, lo:hi]
+
+    def ts(o, i, s1, op0, s2=None, op1=None, r=(), po=None, pi=None, co=None, ci=None, a=()):
+        def fn():
+            out, in0 = ap(o, po, co), ap(i, pi if pi else po, ci)
+            if op1 is None:
+                return V.tensor_scalar(out, in0, s1, None, op0)
+            return V.tensor_scalar(out, in0, s1, s2, op0, op1)
+        run("v", fn, r=tuple(r) + (i,), w=() if a else (o,), a=a)
+
+    def tt(o, x, y, op, po=None, co=None, cx=None, cy=None, a=()):
+        run("v", lambda: V.tensor_tensor(ap(o, po, co), ap(x, po, cx), ap(y, po, cy), op), r=(x, y), w=() if a else (o,), a=a)
+
+    def cp(o, i, po=None, pi=None, co=None, ci=None, a=()):
+        run("v", lambda: V.tensor_copy(ap(o, po, co), ap(i, pi if pi else po, ci)), r=(i,), w=() if a else (o,), a=a)
+
+    def scan(o, d0, d1, c0=None, c1=None, po=None):
+        run("v", lambda: V.tensor_tensor_scan(ap(o, po), ap(d0, po, c0), ap(d1, po, c1), 0.0, OP.mult, OP.add), r=(d0, d1), w=(o,))
+
+    def total_of(o, i, po=None, ci=None):
+        run("v", lambda: V.tensor_reduce(ap(o, po), ap(i, po, ci), X, OP.add), r=(i,), w=(o,))
+
+    def trans(o, i, po=None, ci=None):
+        run("v", lambda: V.transpose(ap(o, po), ap(i, po, ci)), r=(i,), w=(o,))
+
+    def fill(o, c, value, a=()):
+        run("v", lambda: V.memset(ap(o, None, c), float(value)), w=() if a else (o,), a=a)
+
+    def pick(o, olo, ohi, i, ilo, ihi, lst):
+        off = ap(lst)
+        run("v", lambda: V.tensor_copy(words(o, olo, ohi), words(i, ilo, ihi).indirect(off)), r=(i + "c", lst), a=(o + "c",))
+        run("s", lambda: S.activation(plane(o, olo, ohi), plane(i, ilo, ihi).indirect(off), CP), r=(i + "s", lst), a=(o + "s",))
+
+    def quant(o, hi, src, slo, shi):
+        run("v", lambda: V.quantize_mx(T[o + "c"][:, 0:hi], T[o + "s"][:, 0:hi], T[src][:, slo:shi]), r=(src,), a=(o + "c", o + "s"))
+
+    def mm(o, x, y, ylo, yhi):
+        run("t", lambda: TE.matmul_mx(T[o][:, 0:yhi - ylo], T[x + "c"][:, 0:128], T[x + "s"][:, 0:128], T[y + "c"][:, ylo:yhi], T[y + "s"][:, ylo:yhi], True, True),
+            r=(x + "c", x + "s", y + "c", y + "s"), w=(o,))
+
+    def both(o, olo, ohi, i, ilo, ihi):
+        dma("y", [(codes(o, olo, ohi), codes(i, ilo, ihi)), (plane(o, olo, ohi), plane(i, ilo, ihi))], r=(i + "c", i + "s"), a=(o + "c", o + "s"))
+
+    def iota(name, pattern, base, cm):
+        if SCRATCH[name][2] == "int32":
+            run("g", lambda: g.iota(T[name][:], pattern, base, cm), w=(name,))
+        else:
+            run("g", lambda: g.iota(T[name][:], pattern, base, cm, allow_small_or_imprecise_dtypes=True), w=(name,))
+
+    quad = [(32 * b, 32 * b + 32) for b in range(4)]
+    mine = quad[me // 2]
+    half = me % 2
+    later = []
+
+    def gap():
+        if later:
+            later.pop(0)()
+
+    dma("y", [(T.stt[0:16, 1:3], T.st[:, :]), (T.stt[16:32, 0:2], T.st[:, :])], w=("stt",))
+    dma("s", [(T.xb[:, 0:4 * A], T.x[:, :])], a=("xb",))
+    dma("y", [(T.nxa[0:16, :], T.nx[:, :]), (T.nxa[16:32, :], T.nx[:, :])], w=("nxa",))
+    dma("y", [(T.kb[:], T.ky[:, :])], w=("kb",))
+    dma("y", [(T.wb[:], T.w[:, :])], w=("wb",))
+
+    run("v", lambda: V.memset(T.xb[:, 4 * A:512], 0.0), a=("xb",))
+    iota("ip", [[1, 1]], 0, 1)
+    iota("ja", [[0, 2], [-1, A]], A, 0)
+    iota("iw", [[1, 128]], 0, 0)
+    iota("i8", [[-16, 8]], 256 - 16 * me, 1)
+    iota("ik", [[1, 4], [64, 8]], 0, 0)
+    iota("ia", [[1, 8], [0, 4]], 256, -1)
+    iota("ic", [[1, 32]], 256, -1)
+    fill("ct", (0, 32), 0)
+    fill("ct", (32, 64), -RANK, a=("ct",))
+    ts("ip31", "ip", 31, OP.bitwise_and)
+    ts("ip15", "ip", 15, OP.bitwise_and)
+    ts("ip5", "ip", 5, OP.logical_shift_right)
+    cp("af", "ip31")
+    ts("k0", "ip15", float(-GATE), OP.mult)
+    ts("tb", "ip5", 2.0, OP.mult)
+    ts("rowx", "ja", float(TURN), OP.mult, float(A * me), OP.add)
+    fill("one", None, 1)
+    quant("hq0", 128, "xb", 0, 512)
+
+    later.append(lambda: fill("eF", None, 0))
+    later.append(lambda: cp("ipf", "ip"))
+    later.append(lambda: ts("ip3", "ip", 3, OP.bitwise_and))
+    later.append(lambda: run("v", lambda: V.tensor_scalar(T.eF[:, 3:515:4], T.iw[:], T.ipf[:, 0:1], 0.5, OP.is_equal, OP.mult), r=("iw", "ipf"), w=("eF",)))
+    tiles = len(later)
+    later.append(lambda: ts("t4", "ip3", 1.0, OP.mult))
+    later.append(lambda: ts("ia2", "ia", 3, OP.bitwise_and))
+    later.append(lambda: ts("ic2", "ic", 15, OP.bitwise_and))
+    later.append(lambda: ts("nxf", "nxa", 256.0, OP.mult, po=(0, 32)))
+    later.append(lambda: ts("mask", "ia2", 0.0, OP.is_equal, co=(0, 32), a=("mask",)))
+    later.append(lambda: trans("nxt", "nxf", (0, 32)))
+    later.append(lambda: ts("mask", "ic2", 0.0, OP.is_equal, co=(32, 64), a=("mask",)))
+    later.append(lambda: ts("r4", "ip15", 4.0, OP.mult))
+    later.append(lambda: ts("i82", "i8", 112, OP.bitwise_and))
+    later.append(lambda: ts("ku", "ik", T.r4[:, 0:1], OP.add, r=("r4",)))
+    later.append(lambda: ts("mask8", "i82", 0.0, OP.is_equal))
+    later.append(lambda: ts("cl1", "i82", -1.0, OP.mult, float(A + (N - 1) * CAP - RANK * me - A - 1), OP.add, ci=(0, 1)))
+    later.append(lambda: ts("r1", "ip15", 1.0, OP.add))
+    later.append(lambda: tt("cloc", "cl1", "r1", OP.add))
+    tiles = len(later) - tiles
+
+    def table():
+        dma("y", [(T.nrow[0:1, :], T.nxt[0:32, 0:16])], r=("nxt",), w=("nrow",))
+        run("g", lambda: g.partition_broadcast(T.tab[:], T.nrow[0:1, :], 128), r=("nrow",), w=("tab",))
+
+    def unpack(b):
+        quant("e%d" % b, 128, "eF", 3 - b, 3 - b + 512)
+
+    def unpack_keys(parts):
+        for b in parts:
+            mm("d%d" % b, "e%d" % b, "kn", 0, 512)
+            run("s", lambda: S.activation(T.kd[:, b:2048:4], T["d%d" % b][:, 0:512], CP), r=("d%d" % b,), a=("kd",))
+
+    def steps(t):
+        nl = "nl%d" % t
+        for c, v in [((STEP, STEP + 64), 0), ((STEP + 32, STEP + 33), -RANK)]:
+            run("v", lambda: V.memset(ap(nl, None, c), float(v)), r=(nl + "k",), a=(nl + "k",))
+
+    def rows(t, q):
+        n = "_%d" % t
+        if t == 0:
+            ts("bc" + n, "ct", ap("u" + n, q), OP.add, r=("u" + n,), po=q, co=(9, 73))
+        else:
+            nl = "nl%d" % t
+            run("v", lambda: V.tensor_tensor_scan(ap("bc" + n, q), ap("one", q), ap(nl, q, (5, STEP + 64)), 0.0, OP.mult, OP.add), r=("one", nl, nl + "k"), w=("bc" + n,))
+        gap()
+        trans("bt" + n, "bc" + n, q, ci=(9, 73))
+        gap()
+
+    def route(t, q):
+        n = "_%d" % t
+        rows(t, q)
+        for b in quad:
+            ts("be" + n, "bt" + n, 1.0 / RANK, OP.mult, FLOOR, OP.add, po=b, pi=q, a=("be" + n,))
+        tt("pkq" + n, "bt" + n, "rowb" if t else "rowx", OP.add, po=q)
+        gap()
+        ts("ind" + n, "be" + n, T.tb[:, 0:1], OP.is_equal, float(GATE), OP.mult, r=("tb",))
+        for b in quad:
+            cp("pkr" + n, "pkq" + n, po=b, pi=q, a=("pkr" + n,))
+        two = [(0, A), (A, 2 * A)]
+        for c in two:
+            run("v", lambda: V.tensor_tensor_scan(ap("cum" + n, None, c), ap("one", None, (0, A)), ap("ind" + n, None, c), T.k0[:, 0:1], OP.mult, OP.add),
+                r=("one", "ind" + n, "k0"), a=("cum" + n,))
+        gap()
+        for c in two:
+            run("v", lambda: V.tensor_tensor_scan(ap("sp" + n, None, c), ap("pkr" + n, None, c), ap("cum" + n, None, c), 0.0, OP.max, OP.min),
+                r=("pkr" + n, "cum" + n), a=("sp" + n,))
+        gap()
+        for b in range(4):
+            ts("q0" + n, "sp" + n, 0.0, OP.max, po=(0, 32), pi=quad[b], co=(2 * b, 2 * b + 2), ci=(31, 64, 32), a=("q0" + n,))
+        gap()
+        for b in quad:
+            cp("pk%d" % t, "q0" + n, po=b, pi=(0, 32), a=("pk%d" % t,))
+        vl, pk = T["vl%d" % t], T["pk%d" % t]
+        send("apk%d" % t, lambda d: (vl[:, 3 + (me - d) % N:4 + (me - d) % N], pk[:, d:d + 1]), ("pk%d" % t,), NUMBERS)
+        if t > 0:
+            ts("sr" + n, "pk%d" % t, 255, OP.bitwise_and)
+            cp("su" + n, "sr" + n)
+
+    def expect(t, land):
+        cp("vl%d" % t, "pk%d" % t, co=(3, 4), ci=(me, me + 1), a=("vl%d" % t,))
+        arrive("apk%d" % t, per(NUMBERS), ("vl%d" % t,))
+        arrive("aco%d" % t, coming("f%d" % t if t else "x"), (land + "c", land + "s"))
+
+    def depart(t):
+        ld, sd = "ld%d" % t, "sd%d" % t
+        pick(sd, 0, 128, "hq%d" % t, 0, HOME, "su_%d" % t)
+        leave("f%d" % t, sd)
+        both(ld, CAP * me, CAP * me + CAP, sd, CAP * me, CAP * me + CAP)
+        expect(t, ld)
+
+    def stand(t):
+        n, q = "_%d" % t, mine
+        cp("ui" + n, "bc" + n, po=q, ci=(8, 9))
+        ts("ni" + n, "ui" + n, 8, OP.logical_shift_right, po=q)
+        cp("n" + n, "ni" + n, po=q)
+        if t < R:
+            ts("nl%d" % (t + 1), "ni" + n, 256.0, OP.mult, T.af[q[0]:q[1], 0:1], OP.add, r=("af",), po=q, co=(KEPT, KEPT + 1), a=("nl%d" % (t + 1),))
+        dma("y", [(T.nd[t:t + 1, 0:A], ap("n" + n, q))], r=("n" + n,))
+
+    def places(t):
+        n = "_%d" % t
+        for b in quad:
+            cp("li" + n, "bt" + n, po=b, pi=mine, ci=(0, A), a=("li" + n,))
+        ts("lr" + n, "li" + n, 255, OP.bitwise_and)
+        tt("lm" + n, "lr" + n, "mask", OP.mult, cy=(32, 64))
+        scan("lsc" + n, "rst", "lm" + n, c0=(32, 64))
+        cp("lu" + n, "lsc" + n, ci=(15, 32, 16))
+
+    def slots(t):
+        n = "_%d" % t
+        if t == 0:
+            ts("sr_0", "vl0", 255, OP.bitwise_and, ci=(3, 11))
+        tt("vp" + n, "vl%d" % t, "mask8", OP.mult, cx=(3, 11))
+        if t == 0:
+            cp("su_0", "sr_0", co=(me, N), ci=(0, N - me), a=("su_0",))
+        total_of("pkf" + n, "vp" + n)
+        if t == 0 and me:
+            cp("su_0", "sr_0", co=(0, me), ci=(N - me, N), a=("su_0",))
+        cp("pki" + n, "pkf" + n)
+        if t == 0:
+            pick("ld0", 0, 128, "la", 0, N * A, "su_0")
+        ts("vi" + n, "pki" + n, 32512, OP.bitwise_and)
+        ts("ai" + n, "pki" + n, 18, OP.logical_shift_right)
+        ts("vf" + n, "vi" + n, 1.0 / 256, OP.mult)
+        cp("a1" + n, "ai" + n)
+        ts("m%d" % (t % 2), "iw", ap("vf" + n), OP.is_equal, r=("vf" + n,))
+        later.append(lambda: ts("c1" + n, "vf" + n, 4.0, OP.mult, 1024.0, OP.add))
+        later.append(lambda: tt("q1" + n, "cloc", "a1" + n, OP.add))
+        later.append(lambda: ts("i0" + n, "mask", ap("c1" + n), OP.mult, -1024.0, OP.add, r=("c1" + n,)))
+        later.append(lambda: tt("dp" + n, "q1" + n, "vi" + n, OP.subtract))
+        later.append(lambda: ts("oh" + n, "ja", ap("a1" + n), OP.is_equal, r=("a1" + n,), co=(0, 32), ci=(0, 32), a=("oh" + n,)))
+        later.append(lambda: ts("oh" + n, "ja", ap("a1" + n), OP.is_equal, ap("dp" + n), OP.mult, r=("a1" + n, "dp" + n), co=(32, 64), ci=(0, 32), a=("oh" + n,)))
+        later.append(lambda: trans("oht" + n, "oh" + n))
+        while t and later:
+            gap()
+
+    def hop(t):
+        n, ld, qn, sn, dq, hb = "_%d" % t, "ld%d" % t, "qn%d" % t, "sn%d" % t, "dq%d" % t, "hb%d" % t
+        nl, h = "nl%d" % (t + 1), "hq%d" % (t + 1)
+        for j in range(4):
+            mm("z%d" % j, ld, "kj", 128 * j, 128 * j + 128)
+        for j in range(4):
+            tt("p%d" % j + n, "z%d" % j, "m%d" % (t % 2), OP.mult, cx=(0, 128))
+            if j < 3:
+                run("s", lambda: S.activation(ap("j%d" % j + n), ap("p%d" % j + n), CP, accum_out=ap("s4" + n, None, (3 - j, 4 - j))), r=("p%d" % j + n,), w=("j%d" % j + n,), a=("s4" + n,))
+        if t == 0:
+            unpack_keys(REST)
+        for b in range(4):
+            mm("d%d" % b, "e%d" % b, ld, 0, 128)
+        for b in range(4):
+            run("s", lambda: S.activation(T[dq][:, b:512:4], T["d%d" % b][:, 0:128], CP), r=("d%d" % b,), a=(dq,))
+        run("v", lambda: V.tensor_reduce(ap("s4" + n, None, (0, 1)), ap("p3" + n), X, OP.add), r=("p3" + n,), a=("s4" + n,))
+        gap()
+        run("v", lambda: V.tensor_reduce(ap("mx" + n), ap("s4" + n), X, OP.max), r=("s4" + n,), w=("mx" + n,))
+        gap()
+        ts("ne" + n, "s4" + n, ap("mx" + n), OP.not_equal, 1000000.0, OP.mult, r=("mx" + n,))
+        gap()
+        run("v", lambda: V.tensor_tensor_scan(ap("js" + n), T.c1s[:], ap("ne" + n), 0.0, OP.add, OP.min), r=("c1s", "ne" + n), w=("js" + n,))
+        gap()
+        ts("d0" + n, "i0" + n, ap("js" + n, None, (3, 4)), OP.add, 0.0, OP.max, r=("js" + n,))
+        gap()
+        trans("dt" + n, "d0" + n)
+        gap()
+        scan("ds" + n, "rst", "dt" + n)
+        gap()
+
+        def join(b):
+            cp("lf" + n, "ds" + n, po=(0, 32), pi=quad[b], co=(8 * b, 8 * b + 8), ci=(3, 32, 4), a=("lf" + n,))
+        cp("l2u" + n, "ds" + n, ci=(47, 64, 16))
+        join(0)
+        run("v", lambda: V.tensor_tensor(ap("n1" + n), T.tab[:, 0:512].indirect(ap("l2u" + n)), ap("oht" + n, None, (0, 32)), OP.mult), r=("tab", "l2u" + n, "oht" + n), w=("n1" + n,))
+        join(1)
+        for i in range(2):
+            lo, hi = CAP * i, CAP * i + CAP
+            run("v", lambda: V.tensor_tensor_scan(T[sn][:, lo:hi], ap("oht" + n, None, (32 + lo, 32 + hi)), ap("n1" + n, None, (lo, hi)), 0.0, OP.add, OP.add), r=("n1" + n, "oht" + n), a=(sn,))
+        beta = lambda s: (me - s - 1) % N
+        send("adl%d" % t, lambda s: (T[nl][:, 5 + beta(s):6 + beta(s)], T[sn][:, 15 + 16 * (s % 2):16 + 16 * (s % 2)]), (sn,), NUMBERS)
+        arrive("adl%d" % t, per(NUMBERS), (nl,))
+        join(2)
+        join(3)
+        for b in quad:
+            ts("ko" + n, "lf" + n, 4.0, OP.mult, T.t4[0:32, 0:1], OP.add, r=("t4",), po=b, pi=(0, 32), a=("ko" + n,))
+        run("v", lambda: V.tensor_tensor(T[hb][:], T.kd[:, 0:2048].indirect(ap("ko" + n)), T[dq][:], OP.add), r=("kd", "ko" + n, dq), w=(hb,))
+        quant(qn, 128, hb, 0, 512)
+        leave("b%d" % t, qn)
+        both(h, A + 112, HOME, qn, CAP * me, CAP * me + CAP)
+        arrive("are%d" % t, coming("b%d" % t), (h + "c", h + "s"))
+        cp(nl, sn, po=mine, co=(OWN, OWN + 1), ci=(15 + 16 * half, 16 + 16 * half), a=(nl,))
+
+    q = quad[0]
+    hand("x", "c", "hq0")
+    hand("x", "s", "hq0")
+    direct("x", "c", "hq0")
+    ts("u_0", "stt", 256.0, OP.mult, T.af[q[0]:q[1], 0:1], OP.add, r=("af",), po=q, ci=(1, 2))
+    route(0, q)
+    both("la", A * me, A * me + A, "hq0", 0, A)
+    expect(0, "la")
+    while len(later) > tiles:
+        gap()
+    unpack(0)
+    quant("kn", 512, "kb", 0, 2048)
+    unpack_keys((0,))
+    while later:
+        gap()
+    pick("kj", 0, 512, "kn", 0, 512, "ku")
+    table()
+    for b in range(1, 4):
+        unpack(b)
+    unpack_keys(FIRST)
+    fill("c1s", None, 1)
+    fill("rst", None, 1)
+    fill("rst", (0, 32, 4), 0)
+    fill("rst", (32, 64, 16), 0)
+    steps(1)
+    ts("rowb", "ja", float(TURN), OP.mult)
+    slots(0)
+    hop(0)
+    cp("nl1", "u_0", po=mine, pi=q, co=(KEPT, KEPT + 1), a=("nl1",))
+    both("fin", A, 128, "hq0", A, 128)
+    both("hq1", 0, A, "hq0", 0, A)
+    for t in range(1, R + 1):
+        if t < R:
+            route(t, mine)
+            depart(t)
+            stand(t)
+            places(t)
+            pick("hq%d" % (t + 1), 0, A, "hq%d" % t, 0, HOME, "lu_%d" % t)
+            steps(t + 1)
+            if t == 1:
+                cp("n_0", "stt", po=q, ci=(1, 2))
+                dma("y", [(T.nd[0:1, 0:A], ap("n_0", q))], r=("n_0",))
+                quant("wq", 128, "wb", 0, 512)
+            slots(t)
+            hop(t)
+        else:
+            rows(t, mine)
+            places(t)
+            stand(t)
+            pick("fin", 0, A, "hq%d" % t, 0, HOME, "lu_%d" % t)
+            mm("z0", "wq", "fin", 0, 128)
+            dma("y", [(T.oc[:, 0:4 * A], codes("fin", 0, A))], r=("finc",))
+            dma("s", [(T.osc[4 * k:4 * k + 4, 0:A], T.fins[32 * k:32 * k + 4, 0:A]) for k in range(4)], r=("fins",))
+            run("v", lambda: V.tensor_copy(T.yb[:], T.z0[:, 0:A]), r=("z0",), w=("yb",))
+            dma("y", [(T.y[:, :], T.yb[:])], r=("yb",))
+    for sem in total:
+        if waited.get(sem, 0) < total[sem]:
+            g.wait_ge(T.sem[sem], total[sem])

@@ -24,11 +24,11 @@ def _sb(name, cols, ty):
 
 _F, _I, _U, _B, _Q, _S = "float32", "int32", "uint16", "bfloat16", "float8_e4m3fn_x4", "uint8"
 for _n, _c, _t in [
-    ("eF", 516, _B), ("iw", 128, _B), ("ia", 32, _I), ("ia2", 32, _I), ("ic", 32, _I), ("ic2", 32, _I), ("mask", 64, _F),
+    ("eF", 516, _B), ("iw", 128, _B), ("ia", 32, _I), ("ia2", 32, _I), ("ic", 64, _I), ("ic2", 64, _I), ("mask", 96, _F),
     ("ip", 1, _I), ("ip15", 1, _I), ("ip5", 1, _I), ("ip31", 1, _I), ("ip3", 1, _I), ("ipf", 1, _F),
     ("r1", 1, _F), ("k0", 1, _F), ("tb", 1, _F), ("af", 1, _F), ("t4", 1, _F), ("cl1", 1, _F), ("r4", 1, _F),
     ("cloc", 1, _F), ("i8", 8, _I), ("i82", 8, _I), ("mask8", 8, _F), ("ja", 64, _F), ("rowb", 64, _F), ("rowx", 64, _F), ("ct", 64, _F),
-    ("rst", 64, _F), ("one", 73, _F), ("c1s", 4, _F), ("ik", 32, _I),
+    ("rst", 96, _F), ("one", 73, _F), ("ik", 32, _I),
     ("ku", 32, _U), ("stt", 3, _I), ("nxa", 32, _I), ("nxf", 32, _F), ("nxt", 32, _F),
     ("nrow", 512, _F), ("tab", 512, _F), ("xb", 512, _B), ("kb", 2048, _B), ("wb", 512, _B), ("yb", 32, _F), ("m0", 128, _B), ("m1", 128, _B),
     ("kd", 2048, _F),
@@ -63,15 +63,15 @@ def _small(ty, name, cols):
 
 
 for _t in range(R + 1):
-    for _n, _c in [("u", 1), ("bc", 73), ("bt", 64), ("pkq", 64), ("ind", 64), ("cum", 64), ("pkr", 64), ("sp", 64),
+    for _n, _c in [("u", 1), ("bc", 73), ("bt", 64), ("pkq", 64), ("ind", 64), ("cum", 64), ("sp", 64),
                    ("q0", 8), ("n", 1), ("lm", 32), ("lsc", 32), ("vp", 8), ("pkf", 1), ("vf", 1), ("a1", 1),
-                   ("c1", 1), ("i0", 64), ("oh", 64), ("oht", 64), ("q1", 1), ("dp", 1), ("p0", 128), ("p1", 128), ("p2", 128), ("p3", 128),
-                   ("s4", 4), ("mx", 1), ("ne", 4), ("js", 4), ("d0", 64), ("dt", 64), ("ds", 64), ("lf", 32),
-                   ("n1", 32), ("j0", 128), ("j1", 128), ("j2", 128)]:
+                   ("c4", 4), ("g4", 64), ("sc", 64), ("dd", 4), ("oh", 32), ("q1", 1), ("dp", 1), ("p0", 128), ("p1", 128), ("p2", 128), ("p3", 128),
+                   ("s4", 4), ("mx", 1), ("ne", 4), ("js", 4), ("to", 4), ("d0", 64), ("dt", 64), ("lf", 128),
+                   ("j0", 128), ("j1", 128), ("j2", 128)]:
         _small("f", "%s_%d" % (_n, _t), _c)
     for _n, _c in [("li", 32), ("be", 64), ("sr", 8), ("ui", 1), ("ni", 1), ("lr", 32), ("pki", 1), ("vi", 1), ("ai", 1)]:
         _small("i", "%s_%d" % (_n, _t), _c)
-    for _n, _c in [("su", 8), ("lu", 2), ("ko", 32), ("l2u", 2)]:
+    for _n, _c in [("su", 8), ("lu", 2), ("ko", 32), ("of", 4)]:
         _small("u", "%s_%d" % (_n, _t), _c)
 _sb("smf", WIDE["f"][1], _F)
 _sb("smi", WIDE["i"][1], _I)
@@ -316,8 +316,9 @@ def rank_program(g, core, T, topo):
     def cp(o, i, po=None, pi=None, co=None, ci=None, a=()):
         run("v", lambda: V.tensor_copy(ap(o, po, co), ap(i, pi if pi else po, ci)), r=(i,), w=() if a else (o,), a=a)
 
-    def scan(o, d0, d1, c0=None, c1=None, po=None):
-        run("v", lambda: V.tensor_tensor_scan(ap(o, po), ap(d0, po, c0), ap(d1, po, c1), 0.0, OP.mult, OP.add), r=(d0, d1), w=(o,))
+    def scan(o, d0, d1, c0=None, c1=None, po=None, pi=None, co=None, r=(), a=()):
+        run("v", lambda: V.tensor_tensor_scan(ap(o, po, co), ap(d0, pi if pi else po, c0), ap(d1, pi if pi else po, c1), 0.0, OP.mult, OP.add),
+            r=(d0, d1) + tuple(r), w=() if a else (o,), a=a)
 
     def total_of(o, i, po=None, ci=None):
         run("v", lambda: V.tensor_reduce(ap(o, po), ap(i, po, ci), X, OP.add), r=(i,), w=(o,))
@@ -371,7 +372,7 @@ def rank_program(g, core, T, topo):
     iota("i8", [[-16, 8]], 256 - 16 * me, 1)
     iota("ik", [[1, 4], [64, 8]], 0, 0)
     iota("ia", [[1, 8], [0, 4]], 256, -1)
-    iota("ic", [[1, 32]], 256, -1)
+    iota("ic", [[1, 64]], 256, -1)
     fill("ct", (0, 32), 0)
     fill("ct", (32, 64), -RANK, a=("ct",))
     ts("ip31", "ip", 31, OP.bitwise_and)
@@ -395,7 +396,7 @@ def rank_program(g, core, T, topo):
     later.append(lambda: ts("nxf", "nxa", 256.0, OP.mult, po=(0, 32)))
     later.append(lambda: ts("mask", "ia2", 0.0, OP.is_equal, co=(0, 32), a=("mask",)))
     later.append(lambda: trans("nxt", "nxf", (0, 32)))
-    later.append(lambda: ts("mask", "ic2", 0.0, OP.is_equal, co=(32, 64), a=("mask",)))
+    later.append(lambda: ts("mask", "ic2", 0.0, OP.is_equal, co=(32, 96), a=("mask",)))
     later.append(lambda: ts("r4", "ip15", 4.0, OP.mult))
     later.append(lambda: ts("i82", "i8", 112, OP.bitwise_and))
     later.append(lambda: ts("ku", "ik", T.r4[:, 0:1], OP.add, r=("r4",)))
@@ -421,47 +422,54 @@ def rank_program(g, core, T, topo):
         nl = "nl%d" % t
         for c, v in [((STEP, STEP + 64), 0), ((STEP + 32, STEP + 33), -RANK)]:
             run("v", lambda: V.memset(ap(nl, None, c), float(v)), r=(nl + "k",), a=(nl + "k",))
+        fill("c4_%d" % (t - 1), (0, 3), 1, a=("c4_%d" % (t - 1),))
+        if t < R:
+            run("v", lambda: V.memset(T["pk%d" % t][:], 0), w=("pz%d" % t,))
 
     def rows(t, q):
         n = "_%d" % t
-        if t == 0:
-            ts("bc" + n, "ct", ap("u" + n, q), OP.add, r=("u" + n,), po=q, co=(9, 73))
-        else:
-            nl = "nl%d" % t
-            run("v", lambda: V.tensor_tensor_scan(ap("bc" + n, q), ap("one", q), ap(nl, q, (5, STEP + 64)), 0.0, OP.mult, OP.add), r=("one", nl, nl + "k"), w=("bc" + n,))
+        for b in quad:
+            if t == 0:
+                ts("bc" + n, "ct", ap("u" + n, q), OP.add, r=("u" + n,), po=b, pi=q, co=(9, 73), a=("bc" + n,))
+            else:
+                nl = "nl%d" % t
+                scan("bc" + n, "one", nl, c1=(5, STEP + 64), po=b, pi=q, r=(nl + "k",), a=("bc" + n,))
         gap()
-        trans("bt" + n, "bc" + n, q, ci=(9, 73))
+        trans("bt" + n, "bc" + n, ci=(9, 73))
         gap()
 
     def route(t, q):
         n = "_%d" % t
         rows(t, q)
-        for b in quad:
-            ts("be" + n, "bt" + n, 1.0 / RANK, OP.mult, FLOOR, OP.add, po=b, pi=q, a=("be" + n,))
-        tt("pkq" + n, "bt" + n, "rowb" if t else "rowx", OP.add, po=q)
-        gap()
+        ts("be" + n, "bt" + n, 1.0 / RANK, OP.mult, FLOOR, OP.add)
+        tt("pkq" + n, "bt" + n, "rowb" if t else "rowx", OP.add)
         ts("ind" + n, "be" + n, T.tb[:, 0:1], OP.is_equal, float(GATE), OP.mult, r=("tb",))
-        for b in quad:
-            cp("pkr" + n, "pkq" + n, po=b, pi=q, a=("pkr" + n,))
+        gap()
         two = [(0, A), (A, 2 * A)]
         for c in two:
             run("v", lambda: V.tensor_tensor_scan(ap("cum" + n, None, c), ap("one", None, (0, A)), ap("ind" + n, None, c), T.k0[:, 0:1], OP.mult, OP.add),
                 r=("one", "ind" + n, "k0"), a=("cum" + n,))
         gap()
         for c in two:
-            run("v", lambda: V.tensor_tensor_scan(ap("sp" + n, None, c), ap("pkr" + n, None, c), ap("cum" + n, None, c), 0.0, OP.max, OP.min),
-                r=("pkr" + n, "cum" + n), a=("sp" + n,))
+            run("v", lambda: V.tensor_tensor_scan(ap("sp" + n, None, c), ap("pkq" + n, None, c), ap("cum" + n, None, c), 0.0, OP.max, OP.min),
+                r=("pkq" + n, "cum" + n), a=("sp" + n,))
         gap()
-        for b in range(4):
-            ts("q0" + n, "sp" + n, 0.0, OP.max, po=(0, 32), pi=quad[b], co=(2 * b, 2 * b + 2), ci=(31, 64, 32), a=("q0" + n,))
-        gap()
-        for b in quad:
-            cp("pk%d" % t, "q0" + n, po=b, pi=(0, 32), a=("pk%d" % t,))
-        vl, pk = T["vl%d" % t], T["pk%d" % t]
-        send("apk%d" % t, lambda d: (vl[:, 3 + (me - d) % N:4 + (me - d) % N], pk[:, d:d + 1]), ("pk%d" % t,), NUMBERS)
+        pkn = "pk%d" % t
+        if t == 0:
+            for b in range(4):
+                ts("q0" + n, "sp" + n, 0.0, OP.max, po=(0, 32), pi=quad[b], co=(2 * b, 2 * b + 2), ci=(31, 64, 32), a=("q0" + n,))
+            gap()
+            for b in quad:
+                cp(pkn, "q0" + n, po=b, pi=(0, 32), a=(pkn,))
+        else:
+            for b in range(4):
+                ts(pkn, "sp" + n, 0.0, OP.max, r=("pz%d" % t,), po=mine, pi=quad[b], co=(2 * b, 2 * b + 2), ci=(31, 64, 32), a=(pkn,))
+        vl, pk = T["vl%d" % t], T[pkn]
+        send("apk%d" % t, lambda d: (vl[:, 3 + (me - d) % N:4 + (me - d) % N], pk[:, d:d + 1]), (pkn,), NUMBERS)
         if t > 0:
-            ts("sr" + n, "pk%d" % t, 255, OP.bitwise_and)
-            cp("su" + n, "sr" + n)
+            ts("sr" + n, pkn, 255, OP.bitwise_and, po=mine)
+            for b in quad:
+                cp("su" + n, "sr" + n, po=b, pi=mine, a=("su" + n,))
 
     def expect(t, land):
         cp("vl%d" % t, "pk%d" % t, co=(3, 4), ci=(me, me + 1), a=("vl%d" % t,))
@@ -486,8 +494,7 @@ def rank_program(g, core, T, topo):
 
     def places(t):
         n = "_%d" % t
-        for b in quad:
-            cp("li" + n, "bt" + n, po=b, pi=mine, ci=(0, A), a=("li" + n,))
+        cp("li" + n, "bt" + n, ci=(0, A))
         ts("lr" + n, "li" + n, 255, OP.bitwise_and)
         tt("lm" + n, "lr" + n, "mask", OP.mult, cy=(32, 64))
         scan("lsc" + n, "rst", "lm" + n, c0=(32, 64))
@@ -509,15 +516,18 @@ def rank_program(g, core, T, topo):
         ts("vi" + n, "pki" + n, 32512, OP.bitwise_and)
         ts("ai" + n, "pki" + n, 18, OP.logical_shift_right)
         ts("vf" + n, "vi" + n, 1.0 / 256, OP.mult)
-        cp("a1" + n, "ai" + n)
+        ts("c4" + n, "vi" + n, 1.0 / 64, OP.mult, co=(3, 4), a=("c4" + n,))
         ts("m%d" % (t % 2), "iw", ap("vf" + n), OP.is_equal, r=("vf" + n,))
-        later.append(lambda: ts("c1" + n, "vf" + n, 4.0, OP.mult, 1024.0, OP.add))
+        ts("of" + n, "ja", ap("c4" + n, None, (3, 4)), OP.add, -1.0, OP.add, r=("c4" + n,), ci=(A - 4, A))
+        cp("a1" + n, "ai" + n)
+        later.append(lambda: run("v", lambda: V.tensor_tensor(ap("g4" + n), T.tab[:, 0:512].indirect(ap("of" + n)), T.mask[:, 32:96], OP.mult),
+                                 r=("tab", "of" + n, "mask"), w=("g4" + n,)))
         later.append(lambda: tt("q1" + n, "cloc", "a1" + n, OP.add))
-        later.append(lambda: ts("i0" + n, "mask", ap("c1" + n), OP.mult, -1024.0, OP.add, r=("c1" + n,)))
+        later.append(lambda: scan("sc" + n, "rst", "g4" + n, c0=(32, 96)))
         later.append(lambda: tt("dp" + n, "q1" + n, "vi" + n, OP.subtract))
-        later.append(lambda: ts("oh" + n, "ja", ap("a1" + n), OP.is_equal, r=("a1" + n,), co=(0, 32), ci=(0, 32), a=("oh" + n,)))
-        later.append(lambda: ts("oh" + n, "ja", ap("a1" + n), OP.is_equal, ap("dp" + n), OP.mult, r=("a1" + n, "dp" + n), co=(32, 64), ci=(0, 32), a=("oh" + n,)))
-        later.append(lambda: trans("oht" + n, "oh" + n))
+        later.append(lambda: tt("dd" + n, "sc" + n, "sc" + n, OP.subtract, co=(0, 3), cx=(15, 48, 16), cy=(31, 64, 16), a=("dd" + n,)))
+        later.append(lambda: tt("dd" + n, "sc" + n, "dp" + n, OP.add, co=(3, 4), cx=(63, 64), a=("dd" + n,)))
+        later.append(lambda: ts("oh" + n, "ja", ap("a1" + n), OP.is_equal, r=("a1" + n,), ci=(0, 32)))
         while t and later:
             gap()
 
@@ -536,37 +546,29 @@ def rank_program(g, core, T, topo):
             mm("d%d" % b, "e%d" % b, ld, 0, 128)
         for b in range(4):
             run("s", lambda: S.activation(T[dq][:, b:512:4], T["d%d" % b][:, 0:128], CP), r=("d%d" % b,), a=(dq,))
+        gap()
         run("v", lambda: V.tensor_reduce(ap("s4" + n, None, (0, 1)), ap("p3" + n), X, OP.add), r=("p3" + n,), a=("s4" + n,))
+        gap()
         gap()
         run("v", lambda: V.tensor_reduce(ap("mx" + n), ap("s4" + n), X, OP.max), r=("s4" + n,), w=("mx" + n,))
         gap()
-        ts("ne" + n, "s4" + n, ap("mx" + n), OP.not_equal, 1000000.0, OP.mult, r=("mx" + n,))
         gap()
-        run("v", lambda: V.tensor_tensor_scan(ap("js" + n), T.c1s[:], ap("ne" + n), 0.0, OP.add, OP.min), r=("c1s", "ne" + n), w=("js" + n,))
+        ts("ne" + n, "s4" + n, ap("mx" + n), OP.not_equal, r=("mx" + n,))
         gap()
-        ts("d0" + n, "i0" + n, ap("js" + n, None, (3, 4)), OP.add, 0.0, OP.max, r=("js" + n,))
         gap()
+        scan("js" + n, "ne" + n, "c4" + n)
+        scan("to" + n, "ne" + n, "dd" + n)
+        ts("d0" + n, "mask", ap("js" + n, None, (3, 4)), OP.mult, r=("js" + n,), co=(0, 32), ci=(0, 32), a=("d0" + n,))
+        ts("d0" + n, "oh" + n, ap("to" + n, None, (3, 4)), OP.mult, r=("to" + n,), co=(32, 64), a=("d0" + n,))
         trans("dt" + n, "d0" + n)
-        gap()
-        scan("ds" + n, "rst", "dt" + n)
-        gap()
-
-        def join(b):
-            cp("lf" + n, "ds" + n, po=(0, 32), pi=quad[b], co=(8 * b, 8 * b + 8), ci=(3, 32, 4), a=("lf" + n,))
-        cp("l2u" + n, "ds" + n, ci=(47, 64, 16))
-        join(0)
-        run("v", lambda: V.tensor_tensor(ap("n1" + n), T.tab[:, 0:512].indirect(ap("l2u" + n)), ap("oht" + n, None, (0, 32)), OP.mult), r=("tab", "l2u" + n, "oht" + n), w=("n1" + n,))
-        join(1)
-        for i in range(2):
-            lo, hi = CAP * i, CAP * i + CAP
-            run("v", lambda: V.tensor_tensor_scan(T[sn][:, lo:hi], ap("oht" + n, None, (32 + lo, 32 + hi)), ap("n1" + n, None, (lo, hi)), 0.0, OP.add, OP.add), r=("n1" + n, "oht" + n), a=(sn,))
+        scan(sn, "rst", "dt" + n, c0=(32, 64), c1=(32, 64))
         beta = lambda s: (me - s - 1) % N
         send("adl%d" % t, lambda s: (T[nl][:, 5 + beta(s):6 + beta(s)], T[sn][:, 15 + 16 * (s % 2):16 + 16 * (s % 2)]), (sn,), NUMBERS)
         arrive("adl%d" % t, per(NUMBERS), (nl,))
-        join(2)
-        join(3)
+        for b in range(4):
+            scan("lf" + n, "rst", "dt" + n, c0=(0, 32), c1=(0, 32), po=(0, 32), pi=quad[b], co=(32 * b, 32 * b + 32), a=("lf" + n,))
         for b in quad:
-            ts("ko" + n, "lf" + n, 4.0, OP.mult, T.t4[0:32, 0:1], OP.add, r=("t4",), po=b, pi=(0, 32), a=("ko" + n,))
+            ts("ko" + n, "lf" + n, 4.0, OP.mult, T.t4[0:32, 0:1], OP.add, r=("t4",), po=b, pi=(0, 32), ci=(3, 128, 4), a=("ko" + n,))
         run("v", lambda: V.tensor_tensor(T[hb][:], T.kd[:, 0:2048].indirect(ap("ko" + n)), T[dq][:], OP.add), r=("kd", "ko" + n, dq), w=(hb,))
         quant(qn, 128, hb, 0, 512)
         leave("b%d" % t, qn)
@@ -594,10 +596,9 @@ def rank_program(g, core, T, topo):
     for b in range(1, 4):
         unpack(b)
     unpack_keys(FIRST)
-    fill("c1s", None, 1)
     fill("rst", None, 1)
     fill("rst", (0, 32, 4), 0)
-    fill("rst", (32, 64, 16), 0)
+    fill("rst", (32, 96, 16), 0)
     steps(1)
     ts("rowb", "ja", float(TURN), OP.mult)
     slots(0)

@@ -2,17 +2,17 @@ from concourse.bass import DstId, RemoteDMATransfer
 from concourse.mybir import dt, AluOpType, AxisListType, ActivationFunctionType
 
 R, A, P, CAP, N = 3, 32, 512, 16, 8
-HOME = A + N * CAP
-FIRST, REST = (1, 2), (3,)
-OWN, KEPT, STEP = 12, 13, 14
+HALF = N * CAP // 2
+HOME = (N - 1) * CAP + 4 * HALF
+OWN, STEP = 16, 18
 RANK = 32768
 TURN, GATE = 2 ** 18, 2 ** 24
-FLOOR = 2.0 ** -17 - 0.5
-HELPERS = 2
-XKEEP = 4
-KEEP = 1
-HALF = N * CAP // HELPERS
-HAND = 4
+PART = 2.0 ** -19
+LOW = -1e29
+XPLAN = {"c": [(1, (5, 6)), (6, (1, 2))], "s": [(5, (0, 1, 2)), (0, (5, 6)), (2, (3, 4))]}
+FPLAN = {"c": [(5, 1), (2, 2), (0, 3)], "s": []}
+BPLAN = (2, 5, 0)
+TELL = [(1, (3, 4, 5, 6)), (6, (0, 1, 2))]
 LEGS = ["x", "b0", "f1", "b1", "f2", "b2"]
 
 SCRATCH = {}
@@ -26,33 +26,32 @@ _F, _I, _U, _B, _Q, _S = "float32", "int32", "uint16", "bfloat16", "float8_e4m3f
 for _n, _c, _t in [
     ("eF", 516, _B), ("iw", 128, _B), ("ia", 32, _I), ("ia2", 32, _I), ("ic", 64, _I), ("ic2", 64, _I), ("mask", 96, _F),
     ("ip", 1, _I), ("ip15", 1, _I), ("ip5", 1, _I), ("ip31", 1, _I), ("ip3", 1, _I), ("ipf", 1, _F),
-    ("r1", 1, _F), ("k0", 1, _F), ("tb", 1, _F), ("af", 1, _F), ("t4", 1, _F), ("cl1", 1, _F), ("r4", 1, _F),
-    ("cloc", 1, _F), ("i8", 8, _I), ("i82", 8, _I), ("mask8", 8, _F), ("ja", 64, _F), ("rowb", 64, _F), ("rowx", 64, _F), ("ct", 64, _F),
-    ("rst", 96, _F), ("one", 73, _F), ("ik", 32, _I),
+    ("r0", 1, _F), ("r1", 1, _F), ("r2", 1, _F), ("ah", 1, _F), ("k0", 1, _F), ("tb", 1, _F), ("th", 3, _F), ("af", 1, _F), ("t4", 1, _F), ("cl1", 1, _F), ("r4", 1, _F),
+    ("cloc", 1, _F), ("i8", 8, _I), ("i82", 8, _I), ("mask8", 8, _F), ("ja", 32, _F), ("rowb", 32, _F), ("rowx", 32, _F),
+    ("rst", 96, _F), ("one", 40, _F), ("ik", 32, _I), ("pk0", 8, _I), ("vl0", 12, _I),
     ("ku", 32, _U), ("stt", 3, _I), ("nxa", 32, _I), ("nxf", 32, _F), ("nxt", 32, _F),
-    ("nrow", 512, _F), ("tab", 512, _F), ("xb", 512, _B), ("kb", 2048, _B), ("wb", 512, _B), ("yb", 32, _F), ("m0", 128, _B), ("m1", 128, _B),
-    ("kd", 2048, _F),
+    ("nrow", 512, _F), ("tab", 512, _F), ("xb", 512, _B), ("kb", 2048, _B), ("wb", 512, _B), ("yb", 32, _F), ("m", 128, _B),
+    ("kd", 2048, _F), ("hn", 2, _F),
 ]:
     _sb(_n, _c, _t)
 for _n, _c in [("kn", 512), ("kj", 512), ("wq", 128), ("e0", 128), ("e1", 128), ("e2", 128), ("e3", 128), ("hq0", 128), ("fin", 128), ("la", N * A)]:
     _sb(_n + "c", _c, _Q)
     _sb(_n + "s", _c, _S)
 for _t in range(R):
-    for _n, _c in [("sd", 128), ("ld", 128), ("qn", 128)]:
+    for _n in ["sd", "ld"]:
         if _n != "sd" or _t > 0:
-            _sb("%s%dc" % (_n, _t), _c, _Q)
-            _sb("%s%ds" % (_n, _t), _c, _S)
+            _sb("%s%dc" % (_n, _t), 128, _Q)
+            _sb("%s%ds" % (_n, _t), 128, _S)
     _sb("hq%dc" % (_t + 1), HOME, _Q)
     _sb("hq%ds" % (_t + 1), HOME, _S)
-    _sb("pk%d" % _t, 8, _I)
-    _sb("vl%d" % _t, 12, _I)
-    _sb("sn%d" % _t, 32, _F)
-    _sb("nl%d" % (_t + 1), 80, _F)
+    _sb("nl%d" % (_t + 1), STEP + 64, _F)
     _sb("dq%d" % _t, 512, _F)
-    _sb("hb%d" % _t, 512, _B)
-_sb("hxc", A, _Q)
+    _sb("hb%d" % _t, 1024, _B)
 for _l in LEGS:
-    _sb("h%ss" % _l, A if _l == "x" else HALF, _S)
+    if _l[0] != "b":
+        _sb("h%sc" % _l, 2 * CAP, _Q)
+    if _l[0] != "f":
+        _sb("h%ss" % _l, HALF, _S)
 SMALL, WIDE = {}, {"f": ["smf", 0], "i": ["smi", 0], "u": ["smu", 0]}
 
 
@@ -62,14 +61,17 @@ def _small(ty, name, cols):
     w[1] += cols + cols % 2
 
 
+for _n, _c in [("c4", 4), ("kp", 1), ("ne", 4), ("p3", 131), ("s4", 131), ("mx", 131), ("p0", 128), ("p1", 128), ("p2", 128), ("j0", 128), ("j1", 128), ("j2", 128),
+               ("jn", 32), ("maskp", 64), ("clp", 1), ("uf", 1)]:
+    _small("f", _n, _c)
 for _t in range(R + 1):
-    for _n, _c in [("u", 1), ("bc", 73), ("bt", 64), ("pkq", 64), ("ind", 64), ("cum", 64), ("sp", 64),
+    for _n, _c in [("u", 1), ("bc", 40), ("bt", 32), ("pkq", 32), ("ge", 96), ("cum", 64), ("sp", 64),
+                   ("bd", 40), ("b2", 32), ("pk2", 32), ("ge2", 64), ("cu2", 32), ("sp2", 32),
                    ("q0", 8), ("n", 1), ("lm", 32), ("lsc", 32), ("vp", 8), ("pkf", 1), ("vf", 1), ("a1", 1),
-                   ("c4", 4), ("g4", 64), ("sc", 64), ("dd", 4), ("oh", 32), ("q1", 1), ("dp", 1), ("p0", 128), ("p1", 128), ("p2", 128), ("p3", 128),
-                   ("s4", 4), ("mx", 1), ("ne", 4), ("js", 4), ("to", 4), ("d0", 64), ("dt", 64), ("lf", 128),
-                   ("j0", 128), ("j1", 128), ("j2", 128)]:
+                   ("g4", 64), ("sc", 64), ("dd", 4), ("oh", 32), ("dp", 1),
+                   ("js", 4), ("to", 4), ("d0", 32), ("dt", 32), ("d1", 32), ("du", 32), ("lf", 128)]:
         _small("f", "%s_%d" % (_n, _t), _c)
-    for _n, _c in [("li", 32), ("be", 64), ("sr", 8), ("ui", 1), ("ni", 1), ("lr", 32), ("pki", 1), ("vi", 1), ("ai", 1)]:
+    for _n, _c in [("li", 32), ("pk", 8), ("sr", 8), ("ui", 1), ("ni", 1), ("lr", 32), ("pki", 1), ("vi", 1), ("ai", 1)]:
         _small("i", "%s_%d" % (_n, _t), _c)
     for _n, _c in [("su", 8), ("lu", 2), ("ko", 32), ("of", 4)]:
         _small("u", "%s_%d" % (_n, _t), _c)
@@ -80,46 +82,77 @@ for _b in range(4):
     SCRATCH["z%d" % _b] = ("psum", [128, 512], "float32")
     SCRATCH["d%d" % _b] = ("psum", [128, 512], "float32")
 
-SEMAPHORES = ["qv", "qs", "qt", "qg", "ls"] + ["m%d" % _k for _k in range(40)] + ["h" + _l for _l in LEGS]
+SEMAPHORES = ["qv", "qs", "qt", "qg", "ls", "apk0", "hn"] + ["m%d" % _k for _k in range(30)] + ["h" + _l + _k for _l in LEGS for _k in "cs"]
 for _t in range(R):
-    SEMAPHORES += ["apk%d" % _t, "aco%d" % _t, "adl%d" % _t, "are%d" % _t]
+    SEMAPHORES += ["aco%d" % _t, "adl%d" % _t, "arec%d" % _t, "ares%d" % _t]
 
 
-def helpers_of(core, T, topo):
-    can = [c for c in topo.cores_of(core) if T.rank_of(c) is None and all(topo.may_write(c, r) for r in T.cores)]
-    return sorted(can, key=lambda c: topo.die(c) == topo.die(core))[:HELPERS]
+def beside(core, T, topo):
+    return sorted([c for c in topo.cores_of(core) if T.rank_of(c) is None],
+                  key=lambda c: (not all(topo.may_write(c, r) for r in T.cores), topo.die(c) == topo.die(core)))
 
 
-def lanes(n, width=8):
-    calls = []
-    while n:
-        k = 1
-        while 2 * k <= min(n, width):
-            k *= 2
-        w = width // k
-        calls.append([tuple(range(w * i, w * i + w)) for i in range(k)])
-        n -= k
-    return calls
+def reach(s, T, topo):
+    return len(topo.engines(T.cores[s], beside(T.cores[s], T, topo)[0])), len(topo.engines(T.cores[s], T.cores[(s + 1) % N]))
 
 
-def parts(leg, s):
-    out = {"c": [], "s": []}
-    if leg == "x":
-        to = [((s + 1 + b) % N, 0) for b in range(N - 1)]
-        cut = XKEEP + (N - XKEEP) // 2
-        out["c"] = [(None, to[:XKEEP], lanes(XKEEP)), (0, to[XKEEP:cut], lanes(cut - XKEEP)), (1, to[cut:], lanes(N - 1 - cut))]
-        m = (N - 1) // 2
-        out["s"] = [(0, to[:m], lanes(m)), (1, to[m:], lanes(N - 1 - m))]
-        return out
-    to = [((s + i) % N, (s + i) % N) for i in range(1, N)]
-    out["c"].append((None, to, [[(i,) for i in range(6)] + [(6, 7)]]))
-    by = [[e for e in to if e[1] * HELPERS // N == h] for h in range(HELPERS)]
-    own = max(by, key=len)[-KEEP:]
-    out["s"].append((None, own, [[(6, 7)]]))
-    for h in range(HELPERS):
-        l = [e for e in by[h] if e not in own]
-        out["s"].append((h, l, lanes(len(l))))
-    return out
+def block(s, d):
+    return (d // 2 - s // 2) % (N // 2) + N // 2 * ((d - s) % 2)
+
+
+def lanes(n, width):
+    w = [1] * n
+    while n and sum(w) + min(w) <= width:
+        w[w.index(min(w))] *= 2
+    return [tuple(range(sum(w[:i]), sum(w[:i + 1]))) for i in range(n)]
+
+
+def home(s):
+    return (0, HOME - 3 * HALF - A, HOME - 3 * HALF, 0) if s < N // 2 else (2 * HALF, 3 * HALF, HALF, 4 * HALF)
+
+
+PARTS = {}
+
+
+def parts(leg, s, T, topo):
+    if (leg, s) not in PARTS:
+        to, out, by = sorted([d for d in range(N) if d != s], key=lambda d: block(s, d)), {}, beside(T.cores[s], T, topo)
+        on, off = reach(s, T, topo)
+        u = s * 2 // N
+        for k in "cs":
+            if leg == "x":
+                groups, at = [(h, [to[i] for i in l], 0, A, on - off) for h, l in XPLAN[k]], lambda d: 0
+            elif leg[0] == "f":
+                groups, at = [(h, [d for d in to if block(s, d) // 2 == p], 2 * CAP * p, 2 * CAP, on // 4) for h, p in FPLAN[k]], lambda d: block(s, d)
+            else:
+                groups = [(BPLAN[0], [d for d in to if d * 2 // N == u], HALF * u, HALF, on - off)]
+                groups += [(BPLAN[1 + e], [d for d in to if d * 2 // N != u and (d - s) % 2 == e], HALF * (1 - u), HALF, (on - off) // 2) for e in (0, 1)]
+                groups, at = groups if k == "s" else [], lambda d: d
+            own = [d for d in to if not any(d in l[1] for l in groups)]
+            own = [[d for d in own if d * 2 // N == h] for h in (u, 1 - u)] if leg[0] == "b" else [own]
+            out[k] = ([(None, [(d, at(d)) for d in l], 0, 0, 0) for l in own], [(by[h], [(d, at(d)) for d in l], f, w, e) for h, l, f, w, e in groups])
+        PARTS[leg, s] = out
+    return PARTS[leg, s]
+
+
+def write(core, dsts, at, sem, outs, src, topo, total):
+    es = topo.engines(core, dsts[0])
+    total["ls"] = total.get("ls", 0) + len(at)
+    return RemoteDMATransfer(dst_ids=[DstId(rid=topo.addr(c)[0], pnc=topo.addr(c)[1]) for c in dsts], dma_engine_mask=sum(1 << es[k] for k in at), remote_sem=sem, srcs=[src], dsts=outs)
+
+
+def spread(g, core, T, topo, to, sem, land, src, total):
+    at = range(len(topo.engines(core, T.cores[to[0]])))
+    g.remote_dma_fused([write(core, [T.cores[d] for d in to], at, T.sem[sem], [land(d) for d in to], src, topo, total)], local_sem=T.sem["ls"])
+
+
+def told(s):
+    to = sorted([d for d in range(N) if d != s], key=lambda d: block(s, d))
+    return [(h, [to[i] for i in l]) for h, l in TELL]
+
+
+def pair_at(s, d):
+    return 2 + 2 * ((s - d - 1) % N)
 
 
 def landing(leg, s, d):
@@ -127,44 +160,46 @@ def landing(leg, s, d):
         return "la", A * s, A
     if leg[0] == "f":
         return "ld" + leg[1], CAP * s, CAP
-    return "hq%d" % (int(leg[1]) + 1), A + CAP * ((s - d - 1) % N), CAP
+    return "hq%d" % (int(leg[1]) + 1), home(d)[3] + CAP * ((s - d - 1) % N), CAP
 
 
-def sem_of(leg):
-    return "aco0" if leg == "x" else {"f": "aco", "b": "are"}[leg[0]] + leg[1]
+def sem_of(leg, what):
+    return "aco0" if leg == "x" else {"f": "aco", "b": "are" + what}[leg[0]] + leg[1]
 
 
-def issue(g, core, T, topo, leg, s, what, src, first, entries, calls, total):
-    todo = list(entries)
-    for call in calls:
-        tr = []
-        for at in call:
-            d, b = todo.pop(0)
-            dst = T.cores[d]
-            rid, pid, _ = topo.addr(dst)
-            es = topo.engines(core, dst)
-            name, lo, n = landing(leg, s, d)
-            c = CAP * (b - first)
-            o, i = T[name + what][:, lo:lo + n], T[src][:, c:c + n]
-            if what == "c":
-                o, i = o.bitcast(dt.uint8), i.bitcast(dt.uint8)
-            tr.append(RemoteDMATransfer(dst_ids=[DstId(rid=rid, pnc=pid)], dma_engine_mask=sum(1 << es[k] for k in at), remote_sem=T.sem[sem_of(leg)], src=i, dst=o))
-            total["ls"] = total.get("ls", 0) + len(at)
-        g.remote_dma_fused(tr, local_sem=T.sem["ls"])
+def issue(g, core, T, topo, leg, s, what, src, first, entries, total, more=()):
+    def side(name, lo, n):
+        return T[name][:, lo:lo + n].bitcast(dt.uint8) if what == "c" else T[name][:, lo:lo + n]
+
+    def land(d):
+        name, lo, n = landing(leg, s, d)
+        return side(name + what, lo, n)
+    if leg == "x":
+        spread(g, core, T, topo, [d for d, _ in entries], sem_of(leg, what), land, side(src, 0, A), total)
+    else:
+        g.remote_dma_fused(list(more) + [write(core, [T.cores[d]], at, T.sem[sem_of(leg, what)], [land(d)], side(src, CAP * b + first, CAP), topo, total)
+                                         for (d, b), at in zip(entries, lanes(len(entries), reach(s, T, topo)[1]))], local_sem=T.sem["ls"])
 
 
 def helper_program(g, core, T, topo):
     rank = [c for c in topo.cores_of(core) if T.rank_of(c) is not None]
-    if not rank or core not in helpers_of(rank[0], T, topo):
+    if not rank:
         return
-    me, s, total = helpers_of(rank[0], T, topo).index(core), T.rank_of(rank[0]), {}
+    s, total = T.rank_of(rank[0]), {}
+    on, off = reach(s, T, topo)
     for leg in LEGS:
-        g.wait_ge(T.sem["h" + leg], HAND * (2 if leg == "x" else 1))
-        for what, l in parts(leg, s).items():
-            for h, entries, calls in l:
-                if h == me:
-                    issue(g, core, T, topo, leg, s, what, "h" + leg + what, 0 if leg == "x" else N // HELPERS * me, entries, calls, total)
-    g.wait_ge(T.sem["ls"], total["ls"])
+        for h, to in told(s):
+            if leg == LEGS[-1] and core == beside(rank[0], T, topo)[h]:
+                g.wait_ge(T.sem["hn"], on - off)
+                e = to[0] % 2
+                spread(g, core, T, topo, to, "adl%d" % (R - 1), lambda d: T["nl%d" % R][:, pair_at(s, d) + e:pair_at(s, d) + e + 1], T.hn[:, e:e + 1], total)
+        for what, l in parts(leg, s, T, topo).items():
+            for h, entries, first, _, w in l[1]:
+                if h == core:
+                    g.wait_ge(T.sem["h" + leg + what], w)
+                    issue(g, core, T, topo, leg, s, what, "h" + leg + what, -first, entries, total)
+    if total:
+        g.wait_ge(T.sem["ls"], total["ls"])
 
 
 def rank_program(g, core, T, topo):
@@ -172,7 +207,7 @@ def rank_program(g, core, T, topo):
     if me is None:
         helper_program(g, core, T, topo)
         return
-    OP, X, CP = AluOpType, AxisListType.X, ActivationFunctionType.Copy
+    OP, X, CP, ID = AluOpType, AxisListType.X, ActivationFunctionType.Copy, ActivationFunctionType.Identity
     V, S, TE, Y = g.vector, g.scalar, g.tensor, g.sync
     eng = {"v": V, "s": S, "t": TE, "g": g, "y": Y}
     known = {q: {} for q in eng}
@@ -210,6 +245,7 @@ def rank_program(g, core, T, topo):
 
     def run(q, fn, r=(), w=(), a=()):
         before(q, r, w)
+        need(q, [e for k in a for e in rd.get(k, [])])
         sem = "q" + q
         fn().then_inc(T.sem[sem], 1)
         total[sem] = total.get(sem, 0) + 1
@@ -225,57 +261,34 @@ def rank_program(g, core, T, topo):
         done(q, sem, total[sem], r, w, a)
 
     others = [(me + i) % N for i in range(1, N)]
-    helpers = helpers_of(core, T, topo)
-    NUMBERS = [[(i,) for i in range(6)] + [(6, 7)]]
-    per = lambda plan: sum(len(l) for c in plan for l in c)
+    WIN, HELD, NEW, BACK = home(me)
+    near = beside(core, T, topo)
+    on, off = topo.engines(core, near[0]), topo.engines(core, T.cores[others[0]])
+    spare = [k for k in range(len(on)) if on[k] not in off]
+    every = spare + [k for k in range(len(on)) if on[k] in off]
 
-    def send(sem, part, r, plan):
-        before("g", r, ())
-        todo = list(others)
-        for call in plan:
-            tr = []
-            for at in call:
-                d = todo.pop(0)
-                dst = T.cores[d]
-                rid, pid, _ = topo.addr(dst)
-                es = topo.engines(core, dst)
-                o, s = part(d)
-                tr.append(RemoteDMATransfer(dst_ids=[DstId(rid=rid, pnc=pid)], dma_engine_mask=sum(1 << es[k] for k in at), remote_sem=T.sem[sem], src=s, dst=o))
-                total["ls"] = total.get("ls", 0) + len(at)
-            g.remote_dma_fused(tr, local_sem=T.sem["ls"])
+    def handed(leg, what, src, first=0, part=slice(None)):
+        l, sem = parts(leg, me, T, topo)[what][1][part], T.sem["h" + leg + what]
+        side = lambda name, lo, n: T[name + what][:, lo:lo + n].bitcast(dt.uint8) if what == "c" else T[name + what][:, lo:lo + n]
+        if leg == "x":
+            return [write(core, [e[0] for e in l], spare, sem, [side("hx", 0, A)] * len(l), side(src, 0, A), topo, total)]
+        return [write(core, [c], every[h::len(l)][:w], sem, [side("h" + leg, 0, n)], side(src, first + lo, n), topo, total) for h, (c, _, lo, n, w) in enumerate(l)]
 
-    def hand(leg, what, src):
-        before("g", (src + what,), ())
-        free = [k for k in topo.engines(core, helpers[0]) if k not in topo.engines(core, T.cores[others[0]])]
-        tr = []
-        for h, c in enumerate(helpers):
-            rid, pid, _ = topo.addr(c)
-            n, lo = (A, 0) if leg == "x" else (HALF, HALF * h)
-            o, i = T["h" + leg + what][:, 0:n], T[src + what][:, lo:lo + n]
-            if what == "c":
-                o, i = o.bitcast(dt.uint8), i.bitcast(dt.uint8)
-            tr.append(RemoteDMATransfer(dst_ids=[DstId(rid=rid, pnc=pid)], dma_engine_mask=sum(1 << k for k in free[HAND * h:HAND * h + HAND]), remote_sem=T.sem["h" + leg], src=i, dst=o))
-            total["ls"] = total.get("ls", 0) + HAND
-        g.remote_dma_fused(tr, local_sem=T.sem["ls"])
+    def hand(leg, what, src, first=0, part=slice(None), keys=None):
+        before("g", keys or (src + what,), ())
+        g.remote_dma_fused(handed(leg, what, src, first, part), local_sem=T.sem["ls"])
 
-    def direct(leg, what, src):
-        before("g", (src + what,), ())
-        for h, entries, calls in parts(leg, me)[what]:
-            if h is None:
-                issue(g, core, T, topo, leg, me, what, src + what, 0, entries, calls, total)
+    def direct(leg, what, src, part=0, first=0, keys=None, more=()):
+        before("g", keys or (src + what,), ())
+        issue(g, core, T, topo, leg, me, what, src + what, first, parts(leg, me, T, topo)[what][0][part][1], total, more)
 
-    def coming(leg):
+    def coming(leg, both="cs"):
         n = 0
         for s in others:
-            for l in parts(leg, s).values():
-                for h, entries, calls in l:
-                    n += sum(len(at) for (d, b), at in zip(entries, [at for call in calls for at in call]) if d == me)
+            for k in both:
+                for l in parts(leg, s, T, topo)[k]:
+                    n += sum(len(off if leg == "x" else at) for e in l for (d, b), at in zip(e[1], lanes(len(e[1]), len(off))) if d == me)
         return n
-
-    def leave(leg, src):
-        hand(leg, "s", src)
-        direct(leg, "c", src)
-        direct(leg, "s", src)
 
     def arrive(sem, n, keys):
         total[sem] = n
@@ -316,33 +329,35 @@ def rank_program(g, core, T, topo):
     def cp(o, i, po=None, pi=None, co=None, ci=None, a=()):
         run("v", lambda: V.tensor_copy(ap(o, po, co), ap(i, pi if pi else po, ci)), r=(i,), w=() if a else (o,), a=a)
 
-    def scan(o, d0, d1, c0=None, c1=None, po=None, pi=None, co=None, r=(), a=()):
-        run("v", lambda: V.tensor_tensor_scan(ap(o, po, co), ap(d0, pi if pi else po, c0), ap(d1, pi if pi else po, c1), 0.0, OP.mult, OP.add),
+    def scan(o, d0, d1, c0=None, c1=None, po=None, pi=None, co=None, r=(), a=(), first=0.0, ops=(OP.mult, OP.add)):
+        run("v", lambda: V.tensor_tensor_scan(ap(o, po, co), ap(d0, pi if pi else po, c0), ap(d1, pi if pi else po, c1), first, ops[0], ops[1]),
             r=(d0, d1) + tuple(r), w=() if a else (o,), a=a)
-
-    def total_of(o, i, po=None, ci=None):
-        run("v", lambda: V.tensor_reduce(ap(o, po), ap(i, po, ci), X, OP.add), r=(i,), w=(o,))
 
     def trans(o, i, po=None, ci=None):
         run("v", lambda: V.transpose(ap(o, po), ap(i, po, ci)), r=(i,), w=(o,))
 
-    def fill(o, c, value, a=()):
-        run("v", lambda: V.memset(ap(o, None, c), float(value)), w=() if a else (o,), a=a)
+    def act(o, i, scale, bias, po=None, pi=None, co=None, ci=None, a=(), r=()):
+        named = (bias,) if bias in SCRATCH else ()
+        b = ap(bias, pi if pi else po) if named else float(bias)
+        run("s", lambda: S.activation(ap(o, po, co), ap(i, pi if pi else po, ci), ID, bias=b, scale=float(scale)), r=(i,) + tuple(r) + named, w=() if a else (o,), a=a)
 
-    def pick(o, olo, ohi, i, ilo, ihi, lst):
-        off = ap(lst)
-        run("v", lambda: V.tensor_copy(words(o, olo, ohi), words(i, ilo, ihi).indirect(off)), r=(i + "c", lst), a=(o + "c",))
-        run("s", lambda: S.activation(plane(o, olo, ohi), plane(i, ilo, ihi).indirect(off), CP), r=(i + "s", lst), a=(o + "s",))
+    def flat(o, c, n, value, a=()):
+        act(o, "iw", 0, value, co=c, ci=(0, n), a=a)
 
-    def quant(o, hi, src, slo, shi):
-        run("v", lambda: V.quantize_mx(T[o + "c"][:, 0:hi], T[o + "s"][:, 0:hi], T[src][:, slo:shi]), r=(src,), a=(o + "c", o + "s"))
+    def pick(o, olo, ohi, i, ilo, ihi, lst, c=None, r=()):
+        at = ap(lst, None, c)
+        run("v", lambda: V.tensor_copy(words(o, olo, ohi), words(i, ilo, ihi).indirect(at)), r=(i + "c", lst) + r, a=(o + "c",))
+        run("s", lambda: S.activation(plane(o, olo, ohi), plane(i, ilo, ihi).indirect(at), CP), r=(i + "s", lst) + r, a=(o + "s",))
+
+    def quant(o, hi, src, slo, shi, lo=0, r=None, a=()):
+        run("v", lambda: V.quantize_mx(T[o + "c"][:, lo:hi], T[o + "s"][:, lo:hi], T[src][:, slo:shi]), r=r or (src,), a=(o + "c", o + "s") + a)
 
     def mm(o, x, y, ylo, yhi):
         run("t", lambda: TE.matmul_mx(T[o][:, 0:yhi - ylo], T[x + "c"][:, 0:128], T[x + "s"][:, 0:128], T[y + "c"][:, ylo:yhi], T[y + "s"][:, ylo:yhi], True, True),
             r=(x + "c", x + "s", y + "c", y + "s"), w=(o,))
 
-    def both(o, olo, ohi, i, ilo, ihi):
-        dma("y", [(codes(o, olo, ohi), codes(i, ilo, ihi)), (plane(o, olo, ohi), plane(i, ilo, ihi))], r=(i + "c", i + "s"), a=(o + "c", o + "s"))
+    def both(o, olo, ohi, i, ilo, ihi, r=()):
+        dma("y", [(codes(o, olo, ohi), codes(i, ilo, ihi)), (plane(o, olo, ohi), plane(i, ilo, ihi))], r=(i + "c", i + "s") + r, a=(o + "c", o + "s"))
 
     def iota(name, pattern, base, cm):
         if SCRATCH[name][2] == "int32":
@@ -350,9 +365,18 @@ def rank_program(g, core, T, topo):
         else:
             run("g", lambda: g.iota(T[name][:], pattern, base, cm, allow_small_or_imprecise_dtypes=True), w=(name,))
 
+    def mix(*lines):
+        lines = [list(l) for l in lines]
+        while any(lines):
+            for l in lines:
+                if l:
+                    l.pop(0)()
+
     quad = [(32 * b, 32 * b + 32) for b in range(4)]
     mine = quad[me // 2]
     half = me % 2
+    upper = me * 2 // N
+    col = lambda b: (block(me, 2 * b + half), N, N // 2)
     later = []
 
     def gap():
@@ -363,268 +387,281 @@ def rank_program(g, core, T, topo):
     dma("s", [(T.xb[:, 0:4 * A], T.x[:, :])], a=("xb",))
     dma("y", [(T.nxa[0:16, :], T.nx[:, :]), (T.nxa[16:32, :], T.nx[:, :])], w=("nxa",))
     dma("y", [(T.kb[:], T.ky[:, :])], w=("kb",))
-    dma("y", [(T.wb[:], T.w[:, :])], w=("wb",))
-
-    run("v", lambda: V.memset(T.xb[:, 4 * A:512], 0.0), a=("xb",))
-    iota("ip", [[1, 1]], 0, 1)
-    iota("ja", [[0, 2], [-1, A]], A, 0)
-    iota("iw", [[1, 128]], 0, 0)
-    iota("i8", [[-16, 8]], 256 - 16 * me, 1)
-    iota("ik", [[1, 4], [64, 8]], 0, 0)
-    iota("ia", [[1, 8], [0, 4]], 256, -1)
-    iota("ic", [[1, 64]], 256, -1)
-    fill("ct", (0, 32), 0)
-    fill("ct", (32, 64), -RANK, a=("ct",))
-    ts("ip31", "ip", 31, OP.bitwise_and)
-    ts("ip15", "ip", 15, OP.bitwise_and)
-    ts("ip5", "ip", 5, OP.logical_shift_right)
-    cp("af", "ip31")
-    ts("k0", "ip15", float(-GATE), OP.mult)
-    ts("tb", "ip5", 2.0, OP.mult)
-    ts("rowx", "ja", float(TURN), OP.mult, float(A * me), OP.add)
-    fill("one", None, 1)
-    quant("hq0", 128, "xb", 0, 512)
-
-    later.append(lambda: fill("eF", None, 0))
-    later.append(lambda: cp("ipf", "ip"))
-    later.append(lambda: ts("ip3", "ip", 3, OP.bitwise_and))
-    later.append(lambda: run("v", lambda: V.tensor_scalar(T.eF[:, 3:515:4], T.iw[:], T.ipf[:, 0:1], 0.5, OP.is_equal, OP.mult), r=("iw", "ipf"), w=("eF",)))
-    tiles = len(later)
-    later.append(lambda: ts("t4", "ip3", 1.0, OP.mult))
-    later.append(lambda: ts("ia2", "ia", 3, OP.bitwise_and))
-    later.append(lambda: ts("ic2", "ic", 15, OP.bitwise_and))
-    later.append(lambda: ts("nxf", "nxa", 256.0, OP.mult, po=(0, 32)))
-    later.append(lambda: ts("mask", "ia2", 0.0, OP.is_equal, co=(0, 32), a=("mask",)))
-    later.append(lambda: trans("nxt", "nxf", (0, 32)))
-    later.append(lambda: ts("mask", "ic2", 0.0, OP.is_equal, co=(32, 96), a=("mask",)))
-    later.append(lambda: ts("r4", "ip15", 4.0, OP.mult))
-    later.append(lambda: ts("i82", "i8", 112, OP.bitwise_and))
-    later.append(lambda: ts("ku", "ik", T.r4[:, 0:1], OP.add, r=("r4",)))
-    later.append(lambda: ts("mask8", "i82", 0.0, OP.is_equal))
-    later.append(lambda: ts("cl1", "i82", -1.0, OP.mult, float(A + (N - 1) * CAP - RANK * me - A - 1), OP.add, ci=(0, 1)))
-    later.append(lambda: ts("r1", "ip15", 1.0, OP.add))
-    later.append(lambda: tt("cloc", "cl1", "r1", OP.add))
-    tiles = len(later) - tiles
-
-    def table():
-        dma("y", [(T.nrow[0:1, :], T.nxt[0:32, 0:16])], r=("nxt",), w=("nrow",))
-        run("g", lambda: g.partition_broadcast(T.tab[:], T.nrow[0:1, :], 128), r=("nrow",), w=("tab",))
 
     def unpack(b):
         quant("e%d" % b, 128, "eF", 3 - b, 3 - b + 512)
 
-    def unpack_keys(parts):
-        for b in parts:
+    run("v", lambda: V.memset(T.xb[:, 4 * A:512], 0.0), a=("xb",))
+    iota("ip", [[1, 1]], 0, 1)
+    iota("iw", [[1, 128]], 0, 0)
+    iota("ja", [[-1, A]], A, 0)
+    iota("i8", [[-16, 8]], 256 - 16 * me, 1)
+    iota("ik", [[1, 4], [64, 8]], 0, 0)
+    run("v", lambda: V.memset(T.eF[:], 0.0), w=("eF",))
+    ts("ip15", "ip", 15, OP.bitwise_and)
+    ts("ip5", "ip", 5, OP.logical_shift_right)
+    ts("ip31", "ip", 31, OP.bitwise_and)
+    cp("r0", "ip15")
+    ts("tb", "ip5", 2.0 * RANK, OP.mult)
+    cp("ipf", "ip")
+    cp("af", "ip31")
+    run("v", lambda: V.tensor_scalar(T.eF[:, 3:515:4], T.iw[:], T.ipf[:, 0:1], 0.5, OP.is_equal, OP.mult), r=("iw", "ipf"), w=("eF",))
+    ts("ip3", "ip", 3, OP.bitwise_and)
+    quant("hq0", 128, "xb", 0, 512)
+    flat("one", None, 40, 1)
+    act("th", "iw", RANK, "tb", ci=(0, 3))
+    act("rowx", "ja", TURN, A * me)
+    act("k0", "r0", -GATE, 0)
+    act("r4", "r0", 4, 0)
+    for s in (0, N // 2):
+        act("r1", "r0", 1, 1 + home(s)[3] - home(s)[1], po=(CAP * s, CAP * s + HALF), a=("r1",))
+    act("rowb", "ja", TURN, 0)
+    act("ah", "af", 1.0 / CAP, (HELD - WIN) / CAP)
+    flat("rst", None, 96, 1)
+    flat("kp", None, 1, 0)
+    flat("c4", (0, 3), 3, 1, a=("c4",))
+    flat("rst", (0, 32, 4), 8, 0)
+    flat("ne", (0, 1), 1, 0, a=("ne",))
+    flat("p3", (128, 131), 3, 0, a=("p3",))
+    flat("rst", (32, 96, 16), 4, 0)
+    flat("s4", (0, 128), 128, LOW, a=("s4",))
+
+    later.append(lambda: ts("nxf", "nxa", 256.0, OP.mult, po=(0, 32)))
+    later.append(lambda: ts("i82", "i8", 112, OP.bitwise_and))
+    later.append(lambda: trans("nxt", "nxf", (0, 32)))
+    later.append(lambda: ts("ku", "ik", T.r4[:, 0:1], OP.add, r=("r4",)))
+    later.append(lambda: ts("mask8", "i82", 0.0, OP.is_equal))
+    later.append(lambda: ts("cl1", "i82", -1.0, OP.mult, float((N - 1) * CAP - RANK * me - A - 1), OP.add, ci=(0, 1)))
+
+    def unpack_keys(some):
+        for b in some:
             mm("d%d" % b, "e%d" % b, "kn", 0, 512)
             run("s", lambda: S.activation(T.kd[:, b:2048:4], T["d%d" % b][:, 0:512], CP), r=("d%d" % b,), a=("kd",))
 
-    def steps(t):
-        nl = "nl%d" % t
-        for c, v in [((STEP, STEP + 64), 0), ((STEP + 32, STEP + 33), -RANK)]:
-            run("v", lambda: V.memset(ap(nl, None, c), float(v)), r=(nl + "k",), a=(nl + "k",))
-        fill("c4_%d" % (t - 1), (0, 3), 1, a=("c4_%d" % (t - 1),))
-        if t < R:
-            run("v", lambda: V.memset(T["pk%d" % t][:], 0), w=("pz%d" % t,))
+    def ahead(t):
+        for c in (0, 768):
+            run("g", lambda: g.iota(T["hb%d" % t][:, c:c + 256], [[0, 256]], 0, 0, allow_small_or_imprecise_dtypes=True), a=("hb%dz" % t,))
+        flat("nl%d" % (t + 1), (STEP, STEP + 64), 64, 0, a=("nl%dk" % (t + 1),))
 
     def rows(t, q):
         n = "_%d" % t
         for b in quad:
             if t == 0:
-                ts("bc" + n, "ct", ap("u" + n, q), OP.add, r=("u" + n,), po=b, pi=q, co=(9, 73), a=("bc" + n,))
+                ts("bc" + n, "one", ap("u" + n, q), OP.mult, r=("u" + n,), po=b, pi=q, co=(8, 40), ci=(0, A), a=("bc" + n,))
             else:
                 nl = "nl%d" % t
-                scan("bc" + n, "one", nl, c1=(5, STEP + 64), po=b, pi=q, r=(nl + "k",), a=("bc" + n,))
+                scan("bc" + n, "one", nl, c1=(2 + half, STEP + 64, 2), po=b, pi=q, r=(nl + "k",), a=("bc" + n,))
         gap()
-        trans("bt" + n, "bc" + n, ci=(9, 73))
+        trans("bt" + n, "bc" + n, ci=(8, 40))
         gap()
 
     def route(t, q):
         n = "_%d" % t
         rows(t, q)
-        ts("be" + n, "bt" + n, 1.0 / RANK, OP.mult, FLOOR, OP.add)
+        for i in (1, 0, 2):
+            ts("ge" + n, "bt" + n, T.th[:, i:i + 1], OP.is_ge, float(GATE), OP.mult, r=("th",), co=(A * i, A * i + A), a=("ge%d" % i + n,))
         tt("pkq" + n, "bt" + n, "rowb" if t else "rowx", OP.add)
-        ts("ind" + n, "be" + n, T.tb[:, 0:1], OP.is_equal, float(GATE), OP.mult, r=("tb",))
+        for e in (0, 1):
+            c = A * (e ^ half)
+            scan("cum" + n, "ge" + n, "ge" + n, c0=(A * e, A * e + A), c1=(A * e + A, A * e + 2 * A), co=(c, c + A), r=("k0", "ge%d" % e + n, "ge%d" % (e + 1) + n),
+                 a=("cum%d" % c + n,), first=T.k0[:, 0:1], ops=(OP.add, OP.subtract))
         gap()
-        two = [(0, A), (A, 2 * A)]
-        for c in two:
-            run("v", lambda: V.tensor_tensor_scan(ap("cum" + n, None, c), ap("one", None, (0, A)), ap("ind" + n, None, c), T.k0[:, 0:1], OP.mult, OP.add),
-                r=("one", "ind" + n, "k0"), a=("cum" + n,))
+        for e in (0, 1):
+            c = A * (e ^ half)
+            scan("sp" + n, "pkq" + n, "cum" + n, c1=(c, c + A), co=(c, c + A), r=("cum%d" % c + n,), a=("sp" + n,), ops=(OP.max, OP.min))
         gap()
-        for c in two:
-            run("v", lambda: V.tensor_tensor_scan(ap("sp" + n, None, c), ap("pkq" + n, None, c), ap("cum" + n, None, c), 0.0, OP.max, OP.min),
-                r=("pkq" + n, "cum" + n), a=("sp" + n,))
-        gap()
-        pkn = "pk%d" % t
         if t == 0:
             for b in range(4):
-                ts("q0" + n, "sp" + n, 0.0, OP.max, po=(0, 32), pi=quad[b], co=(2 * b, 2 * b + 2), ci=(31, 64, 32), a=("q0" + n,))
+                ts("q0" + n, "sp" + n, 0.0, OP.max, po=(0, 32), pi=quad[b], co=col(b), ci=(31, 64, 32), a=("q0" + n,))
             gap()
             for b in quad:
-                cp(pkn, "q0" + n, po=b, pi=(0, 32), a=(pkn,))
+                cp("pk0", "q0" + n, po=b, pi=(0, 32), a=("pk0",))
+            before("g", ("pk0",), ())
+            g.remote_dma_fused([write(core, [T.cores[d]], at, T.sem.apk0, [T.vl0[:, 3 + (me - d) % N:4 + (me - d) % N]], T.pk0[:, block(me, d):block(me, d) + 1], topo, total)
+                                for d, at in zip(others, lanes(N - 1, len(off)))], local_sem=T.sem["ls"])
         else:
             for b in range(4):
-                ts(pkn, "sp" + n, 0.0, OP.max, r=("pz%d" % t,), po=mine, pi=quad[b], co=(2 * b, 2 * b + 2), ci=(31, 64, 32), a=(pkn,))
-        vl, pk = T["vl%d" % t], T[pkn]
-        send("apk%d" % t, lambda d: (vl[:, 3 + (me - d) % N:4 + (me - d) % N], pk[:, d:d + 1]), (pkn,), NUMBERS)
-        if t > 0:
-            ts("sr" + n, pkn, 255, OP.bitwise_and, po=mine)
+                ts("pk" + n, "sp" + n, 0.0, OP.max, po=mine, pi=quad[b], co=col(b), ci=(31, 64, 32), a=("pk" + n,))
+            ts("sr" + n, "pk" + n, 255, OP.bitwise_and, po=mine)
             for b in quad:
                 cp("su" + n, "sr" + n, po=b, pi=mine, a=("su" + n,))
 
-    def expect(t, land):
-        cp("vl%d" % t, "pk%d" % t, co=(3, 4), ci=(me, me + 1), a=("vl%d" % t,))
-        arrive("apk%d" % t, per(NUMBERS), ("vl%d" % t,))
-        arrive("aco%d" % t, coming("f%d" % t if t else "x"), (land + "c", land + "s"))
-
     def depart(t):
         ld, sd = "ld%d" % t, "sd%d" % t
-        pick(sd, 0, 128, "hq%d" % t, 0, HOME, "su_%d" % t)
-        leave("f%d" % t, sd)
-        both(ld, CAP * me, CAP * me + CAP, sd, CAP * me, CAP * me + CAP)
-        expect(t, ld)
+        pick(sd, 0, 128, "hq%d" % t, WIN, HOME, "su_%d" % t)
+        hand("f%d" % t, "c", sd)
+        direct("f%d" % t, "c", sd)
+        direct("f%d" % t, "s", sd)
+        pick(ld, CAP * me, CAP * me + CAP, "hq%d" % t, WIN, HOME, "su_%d" % t, (0, 1))
+        arrive("aco%d" % t, coming("f%d" % t), (ld + "c", ld + "s"))
 
     def stand(t):
         n, q = "_%d" % t, mine
-        cp("ui" + n, "bc" + n, po=q, ci=(8, 9))
-        ts("ni" + n, "ui" + n, 8, OP.logical_shift_right, po=q)
-        cp("n" + n, "ni" + n, po=q)
-        if t < R:
-            ts("nl%d" % (t + 1), "ni" + n, 256.0, OP.mult, T.af[q[0]:q[1], 0:1], OP.add, r=("af",), po=q, co=(KEPT, KEPT + 1), a=("nl%d" % (t + 1),))
-        dma("y", [(T.nd[t:t + 1, 0:A], ap("n" + n, q))], r=("n" + n,))
+        whole = lambda: cp("ui" + n, "bc" + n, po=q, ci=(8, 9))
+        if t == R:
+            return [whole, lambda: tt("uf", "bc" + n, "ui" + n, OP.subtract, po=q, cx=(8, 9)), lambda: act("n" + n, "uf", 1 / (256 * PART), 0, po=q)]
+
+        def last():
+            cp("n" + n, "ni" + n, po=q)
+            act("kp", "n" + n, 256.0 / CAP * (PART if t == R - 1 else 1), "ah", po=q, a=("kp",))
+        return [whole, lambda: ts("ni" + n, "ui" + n, 8, OP.logical_shift_right, po=q), last]
 
     def places(t):
         n = "_%d" % t
-        cp("li" + n, "bt" + n, ci=(0, A))
-        ts("lr" + n, "li" + n, 255, OP.bitwise_and)
-        tt("lm" + n, "lr" + n, "mask", OP.mult, cy=(32, 64))
-        scan("lsc" + n, "rst", "lm" + n, c0=(32, 64))
-        cp("lu" + n, "lsc" + n, ci=(15, 32, 16))
+        bits = [lambda: cp("li" + n, "bt" + n), lambda: ts("lr" + n, "li" + n, 255, OP.bitwise_and)] if t < R else []
+        return bits + [lambda: tt("lm" + n, ("lr" if t < R else "bt") + n, "mask", OP.mult, cy=(32, 64)),
+                       lambda: scan("lsc" + n, "rst", "lm" + n, c0=(32, 64)), lambda: cp("lu" + n, "lsc" + n, ci=(15, 32, 16))]
+
+    def search(t):
+        n, nl = "_%d" % t, "nl%d" % t
+
+        def gates():
+            for e in (0, 1):
+                ts("ge2" + n, "b2" + n, float(RANK * (me + e)), OP.is_ge, float(GATE), OP.mult, co=(A * e, A * e + A), a=("ge2" + n,))
+            tt("pk2" + n, "b2" + n, "rowb", OP.add)
+        return [lambda: scan("bd" + n, "one", nl, c0=(0, 24), c1=(3, 3 + 48, 2), co=(16, 40), r=(nl + "k",)),
+                lambda: scan("bd" + n, "one", nl, c0=(0, 24), c1=(2, 2 + 48, 2), co=(0, 24), r=(nl + "k",)),
+                lambda: trans("b2" + n, "bd" + n, ci=(8, 40)), gates,
+                lambda: scan("cu2" + n, "ge2" + n, "ge2" + n, c0=(0, A), c1=(A, 2 * A), r=("k0",), first=T.k0[:, 0:1], ops=(OP.add, OP.subtract)),
+                lambda: scan("sp2" + n, "pk2" + n, "cu2" + n, ops=(OP.max, OP.min)),
+                lambda: ts("pki" + n, "sp2" + n, 0.0, OP.max, ci=(A - 1, A))]
 
     def slots(t):
         n = "_%d" % t
-        if t == 0:
-            ts("sr_0", "vl0", 255, OP.bitwise_and, ci=(3, 11))
-        tt("vp" + n, "vl%d" % t, "mask8", OP.mult, cx=(3, 11))
-        if t == 0:
-            cp("su_0", "sr_0", co=(me, N), ci=(0, N - me), a=("su_0",))
-        total_of("pkf" + n, "vp" + n)
-        if t == 0 and me:
-            cp("su_0", "sr_0", co=(0, me), ci=(N - me, N), a=("su_0",))
-        cp("pki" + n, "pkf" + n)
-        if t == 0:
-            pick("ld0", 0, 128, "la", 0, N * A, "su_0")
         ts("vi" + n, "pki" + n, 32512, OP.bitwise_and)
         ts("ai" + n, "pki" + n, 18, OP.logical_shift_right)
         ts("vf" + n, "vi" + n, 1.0 / 256, OP.mult)
-        ts("c4" + n, "vi" + n, 1.0 / 64, OP.mult, co=(3, 4), a=("c4" + n,))
-        ts("m%d" % (t % 2), "iw", ap("vf" + n), OP.is_equal, r=("vf" + n,))
-        ts("of" + n, "ja", ap("c4" + n, None, (3, 4)), OP.add, -1.0, OP.add, r=("c4" + n,), ci=(A - 4, A))
+        ts("c4", "vi" + n, 1.0 / 64, OP.mult, co=(3, 4), a=("c4",))
         cp("a1" + n, "ai" + n)
-        later.append(lambda: run("v", lambda: V.tensor_tensor(ap("g4" + n), T.tab[:, 0:512].indirect(ap("of" + n)), T.mask[:, 32:96], OP.mult),
-                                 r=("tab", "of" + n, "mask"), w=("g4" + n,)))
-        later.append(lambda: tt("q1" + n, "cloc", "a1" + n, OP.add))
-        later.append(lambda: scan("sc" + n, "rst", "g4" + n, c0=(32, 96)))
-        later.append(lambda: tt("dp" + n, "q1" + n, "vi" + n, OP.subtract))
-        later.append(lambda: tt("dd" + n, "sc" + n, "sc" + n, OP.subtract, co=(0, 3), cx=(15, 48, 16), cy=(31, 64, 16), a=("dd" + n,)))
-        later.append(lambda: tt("dd" + n, "sc" + n, "dp" + n, OP.add, co=(3, 4), cx=(63, 64), a=("dd" + n,)))
-        later.append(lambda: ts("oh" + n, "ja", ap("a1" + n), OP.is_equal, r=("a1" + n,), ci=(0, 32)))
-        while t and later:
-            gap()
+        ts("m", "iw", ap("vf" + n), OP.is_equal, r=("vf" + n,))
+        ts("of" + n, "ja", ap("c4", None, (3, 4)), OP.add, -1.0, OP.add, r=("c4",), ci=(A - 4, A))
+        place, unit, by = ("cloc", 1.0, ("mask", None, (32, 96))) if t < R - 1 else ("clp", PART, ("maskp",))
+        ts("dp" + n, "vi" + n, -unit, OP.mult, ap(place), OP.add, r=(place,))
+        return [lambda: run("v", lambda: V.tensor_tensor(ap("g4" + n), T.tab[:, 0:512].indirect(ap("of" + n)), ap(*by), OP.mult),
+                            r=("tab", "of" + n, by[0]), w=("g4" + n,)),
+                lambda: ts("oh" + n, "ja", ap("a1" + n), OP.is_equal, r=("a1" + n,)),
+                lambda: scan("sc" + n, "rst", "g4" + n, c0=(32, 96)),
+                lambda: tt("dd" + n, "sc" + n, "sc" + n, OP.subtract, co=(0, 3), cx=(15, 48, 16), cy=(31, 64, 16), a=("dd" + n,)),
+                lambda: ts("dd" + n, "sc" + n, ap("dp" + n), OP.add, ap("a1" + n), OP.add, r=("dp" + n, "a1" + n), co=(3, 4), ci=(63, 64), a=("dd" + n,))]
 
     def hop(t):
-        n, ld, qn, sn, dq, hb = "_%d" % t, "ld%d" % t, "qn%d" % t, "sn%d" % t, "dq%d" % t, "hb%d" % t
-        nl, h = "nl%d" % (t + 1), "hq%d" % (t + 1)
+        n, ld, dq, hb = "_%d" % t, "ld%d" % t, "dq%d" % t, "hb%d" % t
+        nl, h, leg = "nl%d" % (t + 1), "hq%d" % (t + 1), "b%d" % t
         for j in range(4):
             mm("z%d" % j, ld, "kj", 128 * j, 128 * j + 128)
         for j in range(4):
-            tt("p%d" % j + n, "z%d" % j, "m%d" % (t % 2), OP.mult, cx=(0, 128))
+            tt("p%d" % j, "z%d" % j, "m", OP.mult, cx=(0, 128), co=(0, 128), a=("p%d" % j,))
             if j < 3:
-                run("s", lambda: S.activation(ap("j%d" % j + n), ap("p%d" % j + n), CP, accum_out=ap("s4" + n, None, (3 - j, 4 - j))), r=("p%d" % j + n,), w=("j%d" % j + n,), a=("s4" + n,))
-        if t == 0:
-            unpack_keys(REST)
+                run("s", lambda: S.activation(ap("j%d" % j), ap("p%d" % j), CP, accum_out=ap("s4", None, (130 - j, 131 - j))), r=("p%d" % j,), w=("j%d" % j,), a=("s4",))
         for b in range(4):
             mm("d%d" % b, "e%d" % b, ld, 0, 128)
-        for b in range(4):
-            run("s", lambda: S.activation(T[dq][:, b:512:4], T["d%d" % b][:, 0:128], CP), r=("d%d" % b,), a=(dq,))
-        gap()
-        run("v", lambda: V.tensor_reduce(ap("s4" + n, None, (0, 1)), ap("p3" + n), X, OP.add), r=("p3" + n,), a=("s4" + n,))
-        gap()
-        gap()
-        run("v", lambda: V.tensor_reduce(ap("mx" + n), ap("s4" + n), X, OP.max), r=("s4" + n,), w=("mx" + n,))
-        gap()
-        gap()
-        ts("ne" + n, "s4" + n, ap("mx" + n), OP.not_equal, r=("mx" + n,))
-        gap()
-        gap()
-        scan("js" + n, "ne" + n, "c4" + n)
-        scan("to" + n, "ne" + n, "dd" + n)
-        ts("d0" + n, "mask", ap("js" + n, None, (3, 4)), OP.mult, r=("js" + n,), co=(0, 32), ci=(0, 32), a=("d0" + n,))
-        ts("d0" + n, "oh" + n, ap("to" + n, None, (3, 4)), OP.mult, r=("to" + n,), co=(32, 64), a=("d0" + n,))
+        halve = lambda b: run("s", lambda: S.activation(T[dq][:, b:512:4], T["d%d" % b][:, 0:128], CP), r=("d%d" % b,), a=(dq,))
+        for b in (0, 1):
+            halve(b)
+        scan("mx", "p3", "s4", ops=(OP.add, OP.max))
+        ts("ne", "s4", ap("mx", None, (130, 131)), OP.not_equal, r=("mx",), co=(1, 4), ci=(128, 131), a=("ne",))
+        scan("to" + n, "ne", "dd" + n)
+        scan("js" + n, "ne", "c4")
+        ts("d1" + n, "oh" + n, ap("to" + n, None, (3, 4)), OP.mult, r=("to" + n,))
+        ts("d0" + n, "mask", ap("js" + n, None, (3, 4)), OP.mult, r=("js" + n,), ci=(0, 32))
+        trans("du" + n, "d1" + n)
         trans("dt" + n, "d0" + n)
-        scan(sn, "rst", "dt" + n, c0=(32, 64), c1=(32, 64))
-        beta = lambda s: (me - s - 1) % N
-        send("adl%d" % t, lambda s: (T[nl][:, 5 + beta(s):6 + beta(s)], T[sn][:, 15 + 16 * (s % 2):16 + 16 * (s % 2)]), (sn,), NUMBERS)
-        arrive("adl%d" % t, per(NUMBERS), (nl,))
+        for e in (0, 1):
+            run("s", lambda: S.activation(ap("jn", None, (CAP * e, CAP * e + CAP)), ap("du" + n, None, (CAP * e, CAP * e + CAP)), ID,
+                                          bias=ap("kp") if e == half else 0.0, accum_out=T[nl][:, OWN + e:OWN + e + 1]), r=("du" + n, "kp"), a=("jn", nl, nl + "o"))
+        for b in (2, 3):
+            halve(b)
+        before("g", (nl + "o",), ())
+        if t < R - 1:
+            spread(g, core, T, topo, others, "adl%d" % t, lambda s: T[nl][:, pair_at(me, s):pair_at(me, s) + 2], T[nl][:, OWN:OWN + 2], total)
+        else:
+            g.remote_dma_fused([write(core, [near[c] for c, _ in TELL], spare, T.sem.hn, [T.hn[:, 0:2]] * len(TELL), T[nl][:, OWN:OWN + 2], topo, total)], local_sem=T.sem["ls"])
+        arrive("adl%d" % t, len(off) * (N - 1), (nl,))
         for b in range(4):
             scan("lf" + n, "rst", "dt" + n, c0=(0, 32), c1=(0, 32), po=(0, 32), pi=quad[b], co=(32 * b, 32 * b + 32), a=("lf" + n,))
         for b in quad:
             ts("ko" + n, "lf" + n, 4.0, OP.mult, T.t4[0:32, 0:1], OP.add, r=("t4",), po=b, pi=(0, 32), ci=(3, 128, 4), a=("ko" + n,))
-        run("v", lambda: V.tensor_tensor(T[hb][:], T.kd[:, 0:2048].indirect(ap("ko" + n)), T[dq][:], OP.add), r=("kd", "ko" + n, dq), w=(hb,))
-        quant(qn, 128, hb, 0, 512)
-        leave("b%d" % t, qn)
-        both(h, A + 112, HOME, qn, CAP * me, CAP * me + CAP)
-        arrive("are%d" % t, coming("b%d" % t), (h + "c", h + "s"))
-        cp(nl, sn, po=mine, co=(OWN, OWN + 1), ci=(15 + 16 * half, 16 + 16 * half), a=(nl,))
+        for i in (0, 1):
+            e = i ^ upper
+            lo, c, made = 256 + 256 * e, NEW + HALF * (2 * e - 1), (h + "n%d" % i,)
+            run("v", lambda: V.tensor_tensor(T[hb][:, lo:lo + 256], T.kd[:, 0:2048].indirect(ap("ko" + n, None, (16 * e, 16 * e + 16))), T[dq][:, 256 * e:256 * e + 256], OP.add),
+                r=("kd", "ko" + n, dq), a=(hb + str(e),))
+            quant(h, c + 128, hb, 512 * e, 512 * e + 512, c, (hb + str(e), hb + "z"), made)
+            if i == 0:
+                direct(leg, "c", h, 0, NEW, made, handed(leg, "s", h, NEW, slice(0, 1)))
+            else:
+                hand(leg, "s", h, NEW, slice(1, 3), made)
+                direct(leg, "c", h, 1, NEW, made)
+        for k in "cs":
+            arrive("are%s%d" % (k, t), coming(leg, k), (h + k,))
+        pick(h, HELD, HELD + A, "hq%d" % t, WIN if t else 0, HOME if t else 128, "lu" + n, None, (h + "n0",))
 
     q = quad[0]
+    direct("x", "c", "hq0")
     hand("x", "c", "hq0")
     hand("x", "s", "hq0")
-    direct("x", "c", "hq0")
-    ts("u_0", "stt", 256.0, OP.mult, T.af[q[0]:q[1], 0:1], OP.add, r=("af",), po=q, ci=(1, 2))
-    route(0, q)
     both("la", A * me, A * me + A, "hq0", 0, A)
-    expect(0, "la")
-    while len(later) > tiles:
-        gap()
+    ts("u_0", "stt", 256.0, OP.mult, T.af[q[0]:q[1], 0:1], OP.add, r=("af",), po=q, ci=(1, 2))
     unpack(0)
-    quant("kn", 512, "kb", 0, 2048)
-    unpack_keys((0,))
+    route(0, q)
+    iota("ia", [[1, 8], [0, 4]], 256, -1)
+    iota("ic", [[1, 64]], 256, -1)
+    cp("vl0", "pk0", co=(3, 4), ci=(0, 1), a=("vl0",))
+    arrive("apk0", sum(len(l) for l in lanes(N - 1, len(off))), ("vl0",))
+    arrive("aco0", coming("x"), ("lac", "las"))
     while later:
         gap()
+    act("kp", "u_0", 1.0 / CAP, (HELD - WIN) / CAP, po=mine, pi=q, a=("kp",), r=("kp",))
+    act("r2", "mask8", NEW + CAP * me - BACK - (N - 1) * CAP, "r1", ci=(0, 1))
+    act("cloc", "cl1", 1, "r2")
+    quant("kn", 512, "kb", 0, 2048)
+    unpack(1)
     pick("kj", 0, 512, "kn", 0, 512, "ku")
-    table()
-    for b in range(1, 4):
+    unpack_keys((0, 1))
+    dma("y", [(T.nrow[0:1, :], T.nxt[0:32, 0:16])], r=("nxt",), w=("nrow",))
+    run("g", lambda: g.partition_broadcast(T.tab[:], T.nrow[0:1, :], 128), r=("nrow",), w=("tab",))
+    for b in (2, 3):
         unpack(b)
-    unpack_keys(FIRST)
-    fill("rst", None, 1)
-    fill("rst", (0, 32, 4), 0)
-    fill("rst", (32, 96, 16), 0)
-    steps(1)
-    ts("rowb", "ja", float(TURN), OP.mult)
-    slots(0)
+    unpack_keys((2, 3))
+    ts("ia2", "ia", 3, OP.bitwise_and)
+    ts("ic2", "ic", 15, OP.bitwise_and)
+    cp("t4", "ip3")
+    ts("mask", "ia2", 0.0, OP.is_equal, co=(0, 32), a=("mask",))
+    ts("mask", "ic2", 0.0, OP.is_equal, co=(32, 96), a=("mask",))
+    ts("lu_0", "iw", 16.0, OP.mult, T.r0[:, 0:1], OP.add, r=("r0",), ci=(0, 2))
+    tt("vp_0", "vl0", "mask8", OP.mult, cx=(3, 11))
+    ts("sr_0", "vl0", 255, OP.bitwise_and, ci=(3, 11))
+    run("v", lambda: V.tensor_reduce(ap("pkf_0"), ap("vp_0"), X, OP.add), r=("vp_0",), w=("pkf_0",))
+    cp("su_0", "sr_0", co=(me, N), ci=(0, N - me), a=("su_0",))
+    cp("pki_0", "pkf_0")
+    if me:
+        cp("su_0", "sr_0", co=(0, me), ci=(N - me, N), a=("su_0",))
+    leads = slots(0)
+    mix(leads[:3])
+    pick("ld0", 0, 128, "la", 0, N * A, "su_0")
+    mix(leads[3:])
+    both("fin", A, 128, "hq0", A, 128, ("lac", "las"))
+    dma("y", [(T.wb[:], T.w[:, :])], w=("wb",))
+    ahead(0)
     hop(0)
-    cp("nl1", "u_0", po=mine, pi=q, co=(KEPT, KEPT + 1), a=("nl1",))
-    both("fin", A, 128, "hq0", A, 128)
-    both("hq1", 0, A, "hq0", 0, A)
+    cp("n_0", "stt", po=q, ci=(1, 2))
+    act("maskp", "mask", PART, 0, ci=(32, 96))
+    act("clp", "cloc", 1, RANK * me * (1 - PART))
     for t in range(1, R + 1):
         if t < R:
             route(t, mine)
             depart(t)
-            stand(t)
-            places(t)
-            pick("hq%d" % (t + 1), 0, A, "hq%d" % t, 0, HOME, "lu_%d" % t)
-            steps(t + 1)
-            if t == 1:
-                cp("n_0", "stt", po=q, ci=(1, 2))
-                dma("y", [(T.nd[0:1, 0:A], ap("n_0", q))], r=("n_0",))
-                quant("wq", 128, "wb", 0, 512)
-            slots(t)
+            mix(search(t), stand(t) + places(t))
+            ahead(t)
+            mix(slots(t))
+            dma("y", [(T.nd[k:k + 1, 0:A], ap("n_%d" % k, mine if k else q)) for k in range(t if t > 1 else 0, t + 1)], r=("n_0", "n_%d" % t, "ld%dc" % t))
             hop(t)
         else:
+            quant("wq", 128, "wb", 0, 512)
             rows(t, mine)
-            places(t)
-            stand(t)
-            pick("fin", 0, A, "hq%d" % t, 0, HOME, "lu_%d" % t)
+            mix(places(t), stand(t))
+            dma("y", [(T.nd[t:t + 1, 0:A], ap("n_%d" % t, mine))], r=("n_%d" % t,))
+            pick("fin", 0, A, "hq%d" % t, WIN, HOME, "lu_%d" % t)
             mm("z0", "wq", "fin", 0, 128)
             dma("y", [(T.oc[:, 0:4 * A], codes("fin", 0, A))], r=("finc",))
             dma("s", [(T.osc[4 * k:4 * k + 4, 0:A], T.fins[32 * k:32 * k + 4, 0:A]) for k in range(4)], r=("fins",))

from concourse.bass import DstId, RemoteDMATransfer
from concourse.mybir import dt, AluOpType, AxisListType, ActivationFunctionType

R, A, P, CAP, N = 3, 32, 512, 16, 8
HALF = N * CAP // 2
HOME = (N - 1) * CAP + 4 * HALF
OWN, STEP = 16, 18
RANK = 32768
TURN, GATE = 2 ** 18, 2 ** 24
PART = 2.0 ** -19
LOW = -1e29
XPLAN = {"c": [(1, (5, 6)), (6, (1, 2))], "s": [(5, (0, 1, 2)), (0, (5, 6)), (2, (3, 4))]}
FPLAN = {"c": [(5, 1), (2, 2), (0, 3)], "s": []}
BPLAN = (2, 5, 0)
TELL = [(1, (3, 4, 5, 6)), (6, (0, 1, 2))]
LEGS = ["x", "b0", "f1", "b1", "f2", "b2"]

SCRATCH = {}


def _sb(name, cols, ty):
    SCRATCH[name] = ("sbuf", [128, cols], ty)


_F, _I, _U, _B, _Q, _S = "float32", "int32", "uint16", "bfloat16", "float8_e4m3fn_x4", "uint8"
for _n, _c, _t in [
    ("eF", 516, _B), ("iw", 128, _B), ("ia", 32, _I), ("ia2", 32, _I), ("ic", 64, _I), ("ic2", 64, _I), ("mask", 96, _F),
    ("ip", 1, _I), ("ip15", 1, _I), ("ip5", 1, _I), ("ip31", 1, _I), ("ip3", 1, _I), ("ipf", 1, _F),
    ("r0", 1, _F), ("r1", 1, _F), ("r2", 1, _F), ("ah", 1, _F), ("k0", 1, _F), ("tb", 1, _F), ("th", 3, _F), ("af", 1, _F), ("t4", 1, _F), ("cl1", 1, _F), ("r4", 1, _F),
    ("cloc", 1, _F), ("i8", 8, _I), ("i82", 8, _I), ("mask8", 8, _F), ("ja", 32, _F), ("rowb", 32, _F), ("rowx", 32, _F),
    ("rst", 96, _F), ("one", 40, _F), ("ik", 32, _I), ("pk0", 8, _I), ("vl0", 12, _I),
    ("ku", 32, _U), ("stt", 3, _I), ("nxa", 32, _I), ("nxf", 32, _F), ("nxt", 32, _F),
    ("nrow", 512, _F), ("tab", 512, _F), ("xb", 512, _B), ("kb", 2048, _B), ("wb", 512, _B), ("yb", 32, _F), ("m", 128, _B),
    ("kd", 2048, _F), ("hn", 2, _F),
]:
    _sb(_n, _c, _t)
for _n, _c in [("kn", 512), ("kj", 512), ("wq", 128), ("e0", 128), ("e1", 128), ("e2", 128), ("e3", 128), ("hq0", 128), ("fin", 128), ("la", N * A)]:
    _sb(_n + "c", _c, _Q)
    _sb(_n + "s", _c, _S)
for _t in range(R):
    for _n in ["sd", "ld"]:
        if _n != "sd" or _t > 0:
            _sb("%s%dc" % (_n, _t), 128, _Q)
            _sb("%s%ds" % (_n, _t), 128, _S)
    _sb("hq%dc" % (_t + 1), HOME, _Q)
    _sb("hq%ds" % (_t + 1), HOME, _S)
    _sb("nl%d" % (_t + 1), STEP + 64, _F)
    _sb("dq%d" % _t, 512, _F)
    _sb("hb%d" % _t, 1024, _B)
for _l in LEGS:
    if _l[0] != "b":
        _sb("h%sc" % _l, 2 * CAP, _Q)
    if _l[0] != "f":
        _sb("h%ss" % _l, HALF, _S)
SMALL, WIDE = {}, {"f": ["smf", 0], "i": ["smi", 0], "u": ["smu", 0]}


def _small(ty, name, cols):
    w = WIDE[ty]
    SMALL[name] = (w[0], w[1], w[1] + cols)
    w[1] += cols + cols % 2


for _n, _c in [("c4", 4), ("kp", 1), ("ne", 4), ("p3", 131), ("s4", 131), ("mx", 131), ("p0", 128), ("p1", 128), ("p2", 128), ("j0", 128), ("j1", 128), ("j2", 128),
               ("jn", 32), ("maskp", 64), ("clp", 1), ("uf", 1)]:
    _small("f", _n, _c)
for _t in range(R + 1):
    for _n, _c in [("u", 1), ("bc", 40), ("bt", 32), ("pkq", 32), ("ge", 96), ("cum", 64), ("sp", 64),
                   ("bd", 40), ("b2", 32), ("pk2", 32), ("ge2", 64), ("cu2", 32), ("sp2", 32),
                   ("q0", 8), ("n", 1), ("lm", 32), ("lsc", 32), ("vp", 8), ("pkf", 1), ("vf", 1), ("a1", 1),
                   ("g4", 64), ("sc", 64), ("dd", 4), ("oh", 32), ("dp", 1),
                   ("js", 4), ("to", 4), ("d0", 32), ("dt", 32), ("d1", 32), ("du", 32), ("lf", 128)]:
        _small("f", "%s_%d" % (_n, _t), _c)
    for _n, _c in [("li", 32), ("pk", 8), ("sr", 8), ("ui", 1), ("ni", 1), ("lr", 32), ("pki", 1), ("vi", 1), ("ai", 1)]:
        _small("i", "%s_%d" % (_n, _t), _c)
    for _n, _c in [("su", 8), ("lu", 2), ("ko", 32), ("of", 4)]:
        _small("u", "%s_%d" % (_n, _t), _c)
_sb("smf", WIDE["f"][1], _F)
_sb("smi", WIDE["i"][1], _I)
_sb("smu", WIDE["u"][1], _U)
for _b in range(4):
    SCRATCH["z%d" % _b] = ("psum", [128, 512], "float32")
    SCRATCH["d%d" % _b] = ("psum", [128, 512], "float32")

SEMAPHORES = ["qv", "qs", "qt", "qg", "ls", "apk0", "hn"] + ["m%d" % _k for _k in range(30)] + ["h" + _l + _k for _l in LEGS for _k in "cs"]
for _t in range(R):
    SEMAPHORES += ["aco%d" % _t, "adl%d" % _t, "arec%d" % _t, "ares%d" % _t]


def beside(core, T, topo):
    return sorted([c for c in topo.cores_of(core) if T.rank_of(c) is None],
                  key=lambda c: (not all(topo.may_write(c, r) for r in T.cores), topo.die(c) == topo.die(core)))


def reach(s, T, topo):
    return len(topo.engines(T.cores[s], beside(T.cores[s], T, topo)[0])), len(topo.engines(T.cores[s], T.cores[(s + 1) % N]))


def block(s, d):
    return (d // 2 - s // 2) % (N // 2) + N // 2 * ((d - s) % 2)


def lanes(n, width):
    w = [1] * n
    while n and sum(w) + min(w) <= width:
        w[w.index(min(w))] *= 2
    return [tuple(range(sum(w[:i]), sum(w[:i + 1]))) for i in range(n)]


def home(s):
    return (0, HOME - 3 * HALF - A, HOME - 3 * HALF, 0) if s < N // 2 else (2 * HALF, 3 * HALF, HALF, 4 * HALF)


PARTS = {}


def parts(leg, s, T, topo):
    if (leg, s) not in PARTS:
        to, out, by = sorted([d for d in range(N) if d != s], key=lambda d: block(s, d)), {}, beside(T.cores[s], T, topo)
        on, off = reach(s, T, topo)
        u = s * 2 // N
        for k in "cs":
            if leg == "x":
                groups, at = [(h, [to[i] for i in l], 0, A, on - off) for h, l in XPLAN[k]], lambda d: 0
            elif leg[0] == "f":
                groups, at = [(h, [d for d in to if block(s, d) // 2 == p], 2 * CAP * p, 2 * CAP, on // 4) for h, p in FPLAN[k]], lambda d: block(s, d)
            else:
                groups = [(BPLAN[0], [d for d in to if d * 2 // N == u], HALF * u, HALF, on - off)]
                groups += [(BPLAN[1 + e], [d for d in to if d * 2 // N != u and (d - s) % 2 == e], HALF * (1 - u), HALF, (on - off) // 2) for e in (0, 1)]
                groups, at = groups if k == "s" else [], lambda d: d
            own = [d for d in to if not any(d in l[1] for l in groups)]
            own = [[d for d in own if d * 2 // N == h] for h in (u, 1 - u)] if leg[0] == "b" else [own]
            out[k] = ([(None, [(d, at(d)) for d in l], 0, 0, 0) for l in own], [(by[h], [(d, at(d)) for d in l], f, w, e) for h, l, f, w, e in groups])
        PARTS[leg, s] = out
    return PARTS[leg, s]


def write(core, dsts, at, sem, outs, src, topo, total):
    es = topo.engines(core, dsts[0])
    total["ls"] = total.get("ls", 0) + len(at)
    return RemoteDMATransfer(dst_ids=[DstId(rid=topo.addr(c)[0], pnc=topo.addr(c)[1]) for c in dsts], dma_engine_mask=sum(1 << es[k] for k in at), remote_sem=sem, srcs=[src], dsts=outs)


def spread(g, core, T, topo, to, sem, land, src, total):
    at = range(len(topo.engines(core, T.cores[to[0]])))
    g.remote_dma_fused([write(core, [T.cores[d] for d in to], at, T.sem[sem], [land(d) for d in to], src, topo, total)], local_sem=T.sem["ls"])


def told(s):
    to = sorted([d for d in range(N) if d != s], key=lambda d: block(s, d))
    return [(h, [to[i] for i in l]) for h, l in TELL]


def pair_at(s, d):
    return 2 + 2 * ((s - d - 1) % N)


def landing(leg, s, d):
    if leg == "x":
        return "la", A * s, A
    if leg[0] == "f":
        return "ld" + leg[1], CAP * s, CAP
    return "hq%d" % (int(leg[1]) + 1), home(d)[3] + CAP * ((s - d - 1) % N), CAP


def sem_of(leg, what):
    return "aco0" if leg == "x" else {"f": "aco", "b": "are" + what}[leg[0]] + leg[1]


def issue(g, core, T, topo, leg, s, what, src, first, entries, total, more=()):
    def side(name, lo, n):
        return T[name][:, lo:lo + n].bitcast(dt.uint8) if what == "c" else T[name][:, lo:lo + n]

    def land(d):
        name, lo, n = landing(leg, s, d)
        return side(name + what, lo, n)
    if leg == "x":
        spread(g, core, T, topo, [d for d, _ in entries], sem_of(leg, what), land, side(src, 0, A), total)
    else:
        g.remote_dma_fused(list(more) + [write(core, [T.cores[d]], at, T.sem[sem_of(leg, what)], [land(d)], side(src, CAP * b + first, CAP), topo, total)
                                         for (d, b), at in zip(entries, lanes(len(entries), reach(s, T, topo)[1]))], local_sem=T.sem["ls"])


def helper_program(g, core, T, topo):
    rank = [c for c in topo.cores_of(core) if T.rank_of(c) is not None]
    if not rank:
        return
    s, total = T.rank_of(rank[0]), {}
    on, off = reach(s, T, topo)
    for leg in LEGS:
        for h, to in told(s):
            if leg == LEGS[-1] and core == beside(rank[0], T, topo)[h]:
                g.wait_ge(T.sem["hn"], on - off)
                e = to[0] % 2
                spread(g, core, T, topo, to, "adl%d" % (R - 1), lambda d: T["nl%d" % R][:, pair_at(s, d) + e:pair_at(s, d) + e + 1], T.hn[:, e:e + 1], total)
        for what, l in parts(leg, s, T, topo).items():
            for h, entries, first, _, w in l[1]:
                if h == core:
                    g.wait_ge(T.sem["h" + leg + what], w)
                    issue(g, core, T, topo, leg, s, what, "h" + leg + what, -first, entries, total)
    if total:
        g.wait_ge(T.sem["ls"], total["ls"])


def rank_program(g, core, T, topo):
    me = T.rank_of(core)
    if me is None:
        helper_program(g, core, T, topo)
        return
    OP, X, CP, ID = AluOpType, AxisListType.X, ActivationFunctionType.Copy, ActivationFunctionType.Identity
    V, S, TE, Y = g.vector, g.scalar, g.tensor, g.sync
    eng = {"v": V, "s": S, "t": TE, "g": g, "y": Y}
    known = {q: {} for q in eng}
    total, waited = {}, {}
    wr, rd = {}, {}
    nm = [0]

    def need(q, evs):
        for sem, n, clk in sorted(evs, key=lambda e: -sum(e[2].values())):
            k = known[q]
            if k.get(sem, 0) < n:
                eng[q].wait_ge(T.sem[sem], n)
                k[sem] = n
                waited[sem] = max(waited.get(sem, 0), n)
                for x in clk:
                    k[x] = max(k.get(x, 0), clk[x])

    def before(q, r, w):
        evs = []
        for k in r:
            evs += wr.get(k, [])
        for k in w:
            evs += wr.get(k, []) + rd.get(k, [])
        need(q, evs)

    def done(q, sem, n, r, w, a=()):
        ev = (sem, n, dict(known[q]))
        for k in r:
            rd.setdefault(k, []).append(ev)
        for k in w:
            wr[k] = [ev]
            rd[k] = []
        for k in a:
            wr.setdefault(k, []).append(ev)

    def run(q, fn, r=(), w=(), a=()):
        before(q, r, w)
        need(q, [e for k in a for e in rd.get(k, [])])
        sem = "q" + q
        fn().then_inc(T.sem[sem], 1)
        total[sem] = total.get(sem, 0) + 1
        done(q, sem, total[sem], r, w, a)

    def dma(q, pairs, r=(), w=(), a=()):
        before(q, r, w)
        sem = "m%d" % nm[0]
        nm[0] += 1
        for o, i in pairs:
            eng[q].dma_start(o, i).then_inc(T.sem[sem], 16)
        total[sem] = 16 * len(pairs)
        done(q, sem, total[sem], r, w, a)

    others = [(me + i) % N for i in range(1, N)]
    WIN, HELD, NEW, BACK = home(me)
    near = beside(core, T, topo)
    on, off = topo.engines(core, near[0]), topo.engines(core, T.cores[others[0]])
    spare = [k for k in range(len(on)) if on[k] not in off]
    every = spare + [k for k in range(len(on)) if on[k] in off]

    def handed(leg, what, src, first=0, part=slice(None)):
        l, sem = parts(leg, me, T, topo)[what][1][part], T.sem["h" + leg + what]
        side = lambda name, lo, n: T[name + what][:, lo:lo + n].bitcast(dt.uint8) if what == "c" else T[name + what][:, lo:lo + n]
        if leg == "x":
            return [write(core, [e[0] for e in l], spare, sem, [side("hx", 0, A)] * len(l), side(src, 0, A), topo, total)]
        return [write(core, [c], every[h::len(l)][:w], sem, [side("h" + leg, 0, n)], side(src, first + lo, n), topo, total) for h, (c, _, lo, n, w) in enumerate(l)]

    def hand(leg, what, src, first=0, part=slice(None), keys=None):
        before("g", keys or (src + what,), ())
        g.remote_dma_fused(handed(leg, what, src, first, part), local_sem=T.sem["ls"])

    def direct(leg, what, src, part=0, first=0, keys=None, more=()):
        before("g", keys or (src + what,), ())
        issue(g, core, T, topo, leg, me, what, src + what, first, parts(leg, me, T, topo)[what][0][part][1], total, more)

    def coming(leg, both="cs"):
        n = 0
        for s in others:
            for k in both:
                for l in parts(leg, s, T, topo)[k]:
                    n += sum(len(off if leg == "x" else at) for e in l for (d, b), at in zip(e[1], lanes(len(e[1]), len(off))) if d == me)
        return n

    def arrive(sem, n, keys):
        total[sem] = n
        for k in keys:
            wr.setdefault(k, []).append((sem, n, {}))

    def ap(name, p=None, c=None):
        if name in SMALL:
            buf, lo, hi = SMALL[name]
            c0, c1, st = (0, hi - lo, 1) if c is None else (c if len(c) == 3 else c + (1,))
            cols = slice(lo + c0, lo + c1, st)
        else:
            buf = name
            cols = slice(None) if c is None else (slice(*c))
        rows = slice(None) if p is None else slice(*p)
        return T[buf][rows, cols]

    def codes(name, lo, hi):
        return T[name + "c"][:, lo:hi].bitcast(dt.uint8)

    def words(name, lo, hi):
        return T[name + "c"][:, lo:hi].bitcast(dt.uint32)

    def plane(name, lo, hi):
        return T[name + "s"][:, lo:hi]

    def ts(o, i, s1, op0, s2=None, op1=None, r=(), po=None, pi=None, co=None, ci=None, a=()):
        def fn():
            out, in0 = ap(o, po, co), ap(i, pi if pi else po, ci)
            if op1 is None:
                return V.tensor_scalar(out, in0, s1, None, op0)
            return V.tensor_scalar(out, in0, s1, s2, op0, op1)
        run("v", fn, r=tuple(r) + (i,), w=() if a else (o,), a=a)

    def tt(o, x, y, op, po=None, co=None, cx=None, cy=None, a=()):
        run("v", lambda: V.tensor_tensor(ap(o, po, co), ap(x, po, cx), ap(y, po, cy), op), r=(x, y), w=() if a else (o,), a=a)

    def cp(o, i, po=None, pi=None, co=None, ci=None, a=()):
        run("v", lambda: V.tensor_copy(ap(o, po, co), ap(i, pi if pi else po, ci)), r=(i,), w=() if a else (o,), a=a)

    def scan(o, d0, d1, c0=None, c1=None, po=None, pi=None, co=None, r=(), a=(), first=0.0, ops=(OP.mult, OP.add)):
        run("v", lambda: V.tensor_tensor_scan(ap(o, po, co), ap(d0, pi if pi else po, c0), ap(d1, pi if pi else po, c1), first, ops[0], ops[1]),
            r=(d0, d1) + tuple(r), w=() if a else (o,), a=a)

    def trans(o, i, po=None, ci=None):
        run("v", lambda: V.transpose(ap(o, po), ap(i, po, ci)), r=(i,), w=(o,))

    def act(o, i, scale, bias, po=None, pi=None, co=None, ci=None, a=(), r=()):
        named = (bias,) if bias in SCRATCH else ()
        b = ap(bias, pi if pi else po) if named else float(bias)
        run("s", lambda: S.activation(ap(o, po, co), ap(i, pi if pi else po, ci), ID, bias=b, scale=float(scale)), r=(i,) + tuple(r) + named, w=() if a else (o,), a=a)

    def flat(o, c, n, value, a=()):
        act(o, "iw", 0, value, co=c, ci=(0, n), a=a)

    def pick(o, olo, ohi, i, ilo, ihi, lst, c=None, r=()):
        at = ap(lst, None, c)
        run("v", lambda: V.tensor_copy(words(o, olo, ohi), words(i, ilo, ihi).indirect(at)), r=(i + "c", lst) + r, a=(o + "c",))
        run("s", lambda: S.activation(plane(o, olo, ohi), plane(i, ilo, ihi).indirect(at), CP), r=(i + "s", lst) + r, a=(o + "s",))

    def quant(o, hi, src, slo, shi, lo=0, r=None, a=()):
        run("v", lambda: V.quantize_mx(T[o + "c"][:, lo:hi], T[o + "s"][:, lo:hi], T[src][:, slo:shi]), r=r or (src,), a=(o + "c", o + "s") + a)

    def mm(o, x, y, ylo, yhi):
        run("t", lambda: TE.matmul_mx(T[o][:, 0:yhi - ylo], T[x + "c"][:, 0:128], T[x + "s"][:, 0:128], T[y + "c"][:, ylo:yhi], T[y + "s"][:, ylo:yhi], True, True),
            r=(x + "c", x + "s", y + "c", y + "s"), w=(o,))

    def both(o, olo, ohi, i, ilo, ihi, r=()):
        dma("y", [(codes(o, olo, ohi), codes(i, ilo, ihi)), (plane(o, olo, ohi), plane(i, ilo, ihi))], r=(i + "c", i + "s") + r, a=(o + "c", o + "s"))

    def iota(name, pattern, base, cm):
        if SCRATCH[name][2] == "int32":
            run("g", lambda: g.iota(T[name][:], pattern, base, cm), w=(name,))
        else:
            run("g", lambda: g.iota(T[name][:], pattern, base, cm, allow_small_or_imprecise_dtypes=True), w=(name,))

    def mix(*lines):
        lines = [list(l) for l in lines]
        while any(lines):
            for l in lines:
                if l:
                    l.pop(0)()

    quad = [(32 * b, 32 * b + 32) for b in range(4)]
    mine = quad[me // 2]
    half = me % 2
    upper = me * 2 // N
    col = lambda b: (block(me, 2 * b + half), N, N // 2)
    later = []

    def gap():
        if later:
            later.pop(0)()

    dma("y", [(T.stt[0:16, 1:3], T.st[:, :]), (T.stt[16:32, 0:2], T.st[:, :])], w=("stt",))
    dma("s", [(T.xb[:, 0:4 * A], T.x[:, :])], a=("xb",))
    dma("y", [(T.nxa[0:16, :], T.nx[:, :]), (T.nxa[16:32, :], T.nx[:, :])], w=("nxa",))
    dma("y", [(T.kb[:], T.ky[:, :])], w=("kb",))

    def unpack(b):
        quant("e%d" % b, 128, "eF", 3 - b, 3 - b + 512)

    run("v", lambda: V.memset(T.xb[:, 4 * A:512], 0.0), a=("xb",))
    iota("ip", [[1, 1]], 0, 1)
    iota("iw", [[1, 128]], 0, 0)
    iota("ja", [[-1, A]], A, 0)
    iota("i8", [[-16, 8]], 256 - 16 * me, 1)
    iota("ik", [[1, 4], [64, 8]], 0, 0)
    run("v", lambda: V.memset(T.eF[:], 0.0), w=("eF",))
    ts("ip15", "ip", 15, OP.bitwise_and)
    ts("ip5", "ip", 5, OP.logical_shift_right)
    ts("ip31", "ip", 31, OP.bitwise_and)
    cp("r0", "ip15")
    ts("tb", "ip5", 2.0 * RANK, OP.mult)
    cp("ipf", "ip")
    cp("af", "ip31")
    run("v", lambda: V.tensor_scalar(T.eF[:, 3:515:4], T.iw[:], T.ipf[:, 0:1], 0.5, OP.is_equal, OP.mult), r=("iw", "ipf"), w=("eF",))
    ts("ip3", "ip", 3, OP.bitwise_and)
    quant("hq0", 128, "xb", 0, 512)
    flat("one", None, 40, 1)
    act("th", "iw", RANK, "tb", ci=(0, 3))
    act("rowx", "ja", TURN, A * me)
    act("k0", "r0", -GATE, 0)
    act("r4", "r0", 4, 0)
    for s in (0, N // 2):
        act("r1", "r0", 1, 1 + home(s)[3] - home(s)[1], po=(CAP * s, CAP * s + HALF), a=("r1",))
    act("rowb", "ja", TURN, 0)
    act("ah", "af", 1.0 / CAP, (HELD - WIN) / CAP)
    flat("rst", None, 96, 1)
    flat("kp", None, 1, 0)
    flat("c4", (0, 3), 3, 1, a=("c4",))
    flat("rst", (0, 32, 4), 8, 0)
    flat("ne", (0, 1), 1, 0, a=("ne",))
    flat("p3", (128, 131), 3, 0, a=("p3",))
    flat("rst", (32, 96, 16), 4, 0)
    flat("s4", (0, 128), 128, LOW, a=("s4",))

    later.append(lambda: ts("nxf", "nxa", 256.0, OP.mult, po=(0, 32)))
    later.append(lambda: ts("i82", "i8", 112, OP.bitwise_and))
    later.append(lambda: trans("nxt", "nxf", (0, 32)))
    later.append(lambda: ts("ku", "ik", T.r4[:, 0:1], OP.add, r=("r4",)))
    later.append(lambda: ts("mask8", "i82", 0.0, OP.is_equal))
    later.append(lambda: ts("cl1", "i82", -1.0, OP.mult, float((N - 1) * CAP - RANK * me - A - 1), OP.add, ci=(0, 1)))

    def unpack_keys(some):
        for b in some:
            mm("d%d" % b, "e%d" % b, "kn", 0, 512)
            run("s", lambda: S.activation(T.kd[:, b:2048:4], T["d%d" % b][:, 0:512], CP), r=("d%d" % b,), a=("kd",))

    def ahead(t):
        for c in (0, 768):
            run("g", lambda: g.iota(T["hb%d" % t][:, c:c + 256], [[0, 256]], 0, 0, allow_small_or_imprecise_dtypes=True), a=("hb%dz" % t,))
        flat("nl%d" % (t + 1), (STEP, STEP + 64), 64, 0, a=("nl%dk" % (t + 1),))

    def rows(t, q):
        n = "_%d" % t
        for b in quad:
            if t == 0:
                ts("bc" + n, "one", ap("u" + n, q), OP.mult, r=("u" + n,), po=b, pi=q, co=(8, 40), ci=(0, A), a=("bc" + n,))
            else:
                nl = "nl%d" % t
                scan("bc" + n, "one", nl, c1=(2 + half, STEP + 64, 2), po=b, pi=q, r=(nl + "k",), a=("bc" + n,))
        gap()
        trans("bt" + n, "bc" + n, ci=(8, 40))
        gap()

    def route(t, q):
        n = "_%d" % t
        rows(t, q)
        for i in (1, 0, 2):
            ts("ge" + n, "bt" + n, T.th[:, i:i + 1], OP.is_ge, float(GATE), OP.mult, r=("th",), co=(A * i, A * i + A), a=("ge%d" % i + n,))
        tt("pkq" + n, "bt" + n, "rowb" if t else "rowx", OP.add)
        for e in (0, 1):
            c = A * (e ^ half)
            scan("cum" + n, "ge" + n, "ge" + n, c0=(A * e, A * e + A), c1=(A * e + A, A * e + 2 * A), co=(c, c + A), r=("k0", "ge%d" % e + n, "ge%d" % (e + 1) + n),
                 a=("cum%d" % c + n,), first=T.k0[:, 0:1], ops=(OP.add, OP.subtract))
        gap()
        for e in (0, 1):
            c = A * (e ^ half)
            scan("sp" + n, "pkq" + n, "cum" + n, c1=(c, c + A), co=(c, c + A), r=("cum%d" % c + n,), a=("sp" + n,), ops=(OP.max, OP.min))
        gap()
        if t == 0:
            for b in range(4):
                ts("q0" + n, "sp" + n, 0.0, OP.max, po=(0, 32), pi=quad[b], co=col(b), ci=(31, 64, 32), a=("q0" + n,))
            gap()
            for b in quad:
                cp("pk0", "q0" + n, po=b, pi=(0, 32), a=("pk0",))
            before("g", ("pk0",), ())
            g.remote_dma_fused([write(core, [T.cores[d]], at, T.sem.apk0, [T.vl0[:, 3 + (me - d) % N:4 + (me - d) % N]], T.pk0[:, block(me, d):block(me, d) + 1], topo, total)
                                for d, at in zip(others, lanes(N - 1, len(off)))], local_sem=T.sem["ls"])
        else:
            for b in range(4):
                ts("pk" + n, "sp" + n, 0.0, OP.max, po=mine, pi=quad[b], co=col(b), ci=(31, 64, 32), a=("pk" + n,))
            ts("sr" + n, "pk" + n, 255, OP.bitwise_and, po=mine)
            for b in quad:
                cp("su" + n, "sr" + n, po=b, pi=mine, a=("su" + n,))

    def depart(t):
        ld, sd = "ld%d" % t, "sd%d" % t
        pick(sd, 0, 128, "hq%d" % t, WIN, HOME, "su_%d" % t)
        hand("f%d" % t, "c", sd)
        direct("f%d" % t, "c", sd)
        direct("f%d" % t, "s", sd)
        pick(ld, CAP * me, CAP * me + CAP, "hq%d" % t, WIN, HOME, "su_%d" % t, (0, 1))
        arrive("aco%d" % t, coming("f%d" % t), (ld + "c", ld + "s"))

    def stand(t):
        n, q = "_%d" % t, mine
        whole = lambda: cp("ui" + n, "bc" + n, po=q, ci=(8, 9))
        if t == R:
            return [whole, lambda: tt("uf", "bc" + n, "ui" + n, OP.subtract, po=q, cx=(8, 9)), lambda: act("n" + n, "uf", 1 / (256 * PART), 0, po=q)]

        def last():
            cp("n" + n, "ni" + n, po=q)
            act("kp", "n" + n, 256.0 / CAP * (PART if t == R - 1 else 1), "ah", po=q, a=("kp",))
        return [whole, lambda: ts("ni" + n, "ui" + n, 8, OP.logical_shift_right, po=q), last]

    def places(t):
        n = "_%d" % t
        bits = [lambda: cp("li" + n, "bt" + n), lambda: ts("lr" + n, "li" + n, 255, OP.bitwise_and)] if t < R else []
        return bits + [lambda: tt("lm" + n, ("lr" if t < R else "bt") + n, "mask", OP.mult, cy=(32, 64)),
                       lambda: scan("lsc" + n, "rst", "lm" + n, c0=(32, 64)), lambda: cp("lu" + n, "lsc" + n, ci=(15, 32, 16))]

    def search(t):
        n, nl = "_%d" % t, "nl%d" % t

        def gates():
            for e in (0, 1):
                ts("ge2" + n, "b2" + n, float(RANK * (me + e)), OP.is_ge, float(GATE), OP.mult, co=(A * e, A * e + A), a=("ge2" + n,))
            tt("pk2" + n, "b2" + n, "rowb", OP.add)
        return [lambda: scan("bd" + n, "one", nl, c0=(0, 24), c1=(3, 3 + 48, 2), co=(16, 40), r=(nl + "k",)),
                lambda: scan("bd" + n, "one", nl, c0=(0, 24), c1=(2, 2 + 48, 2), co=(0, 24), r=(nl + "k",)),
                lambda: trans("b2" + n, "bd" + n, ci=(8, 40)), gates,
                lambda: scan("cu2" + n, "ge2" + n, "ge2" + n, c0=(0, A), c1=(A, 2 * A), r=("k0",), first=T.k0[:, 0:1], ops=(OP.add, OP.subtract)),
                lambda: scan("sp2" + n, "pk2" + n, "cu2" + n, ops=(OP.max, OP.min)),
                lambda: ts("pki" + n, "sp2" + n, 0.0, OP.max, ci=(A - 1, A))]

    def slots(t):
        n = "_%d" % t
        ts("vi" + n, "pki" + n, 32512, OP.bitwise_and)
        ts("ai" + n, "pki" + n, 18, OP.logical_shift_right)
        ts("vf" + n, "vi" + n, 1.0 / 256, OP.mult)
        ts("c4", "vi" + n, 1.0 / 64, OP.mult, co=(3, 4), a=("c4",))
        cp("a1" + n, "ai" + n)
        ts("m", "iw", ap("vf" + n), OP.is_equal, r=("vf" + n,))
        ts("of" + n, "ja", ap("c4", None, (3, 4)), OP.add, -1.0, OP.add, r=("c4",), ci=(A - 4, A))
        place, unit, by = ("cloc", 1.0, ("mask", None, (32, 96))) if t < R - 1 else ("clp", PART, ("maskp",))
        ts("dp" + n, "vi" + n, -unit, OP.mult, ap(place), OP.add, r=(place,))
        return [lambda: run("v", lambda: V.tensor_tensor(ap("g4" + n), T.tab[:, 0:512].indirect(ap("of" + n)), ap(*by), OP.mult),
                            r=("tab", "of" + n, by[0]), w=("g4" + n,)),
                lambda: ts("oh" + n, "ja", ap("a1" + n), OP.is_equal, r=("a1" + n,)),
                lambda: scan("sc" + n, "rst", "g4" + n, c0=(32, 96)),
                lambda: tt("dd" + n, "sc" + n, "sc" + n, OP.subtract, co=(0, 3), cx=(15, 48, 16), cy=(31, 64, 16), a=("dd" + n,)),
                lambda: ts("dd" + n, "sc" + n, ap("dp" + n), OP.add, ap("a1" + n), OP.add, r=("dp" + n, "a1" + n), co=(3, 4), ci=(63, 64), a=("dd" + n,))]

    def hop(t):
        n, ld, dq, hb = "_%d" % t, "ld%d" % t, "dq%d" % t, "hb%d" % t
        nl, h, leg = "nl%d" % (t + 1), "hq%d" % (t + 1), "b%d" % t
        for j in range(4):
            mm("z%d" % j, ld, "kj", 128 * j, 128 * j + 128)
        for j in range(4):
            tt("p%d" % j, "z%d" % j, "m", OP.mult, cx=(0, 128), co=(0, 128), a=("p%d" % j,))
            if j < 3:
                run("s", lambda: S.activation(ap("j%d" % j), ap("p%d" % j), CP, accum_out=ap("s4", None, (130 - j, 131 - j))), r=("p%d" % j,), w=("j%d" % j,), a=("s4",))
        for b in range(4):
            mm("d%d" % b, "e%d" % b, ld, 0, 128)
        halve = lambda b: run("s", lambda: S.activation(T[dq][:, b:512:4], T["d%d" % b][:, 0:128], CP), r=("d%d" % b,), a=(dq,))
        for b in (0, 1):
            halve(b)
        scan("mx", "p3", "s4", ops=(OP.add, OP.max))
        ts("ne", "s4", ap("mx", None, (130, 131)), OP.not_equal, r=("mx",), co=(1, 4), ci=(128, 131), a=("ne",))
        scan("to" + n, "ne", "dd" + n)
        scan("js" + n, "ne", "c4")
        ts("d1" + n, "oh" + n, ap("to" + n, None, (3, 4)), OP.mult, r=("to" + n,))
        ts("d0" + n, "mask", ap("js" + n, None, (3, 4)), OP.mult, r=("js" + n,), ci=(0, 32))
        trans("du" + n, "d1" + n)
        trans("dt" + n, "d0" + n)
        for e in (0, 1):
            run("s", lambda: S.activation(ap("jn", None, (CAP * e, CAP * e + CAP)), ap("du" + n, None, (CAP * e, CAP * e + CAP)), ID,
                                          bias=ap("kp") if e == half else 0.0, accum_out=T[nl][:, OWN + e:OWN + e + 1]), r=("du" + n, "kp"), a=("jn", nl, nl + "o"))
        for b in (2, 3):
            halve(b)
        before("g", (nl + "o",), ())
        if t < R - 1:
            spread(g, core, T, topo, others, "adl%d" % t, lambda s: T[nl][:, pair_at(me, s):pair_at(me, s) + 2], T[nl][:, OWN:OWN + 2], total)
        else:
            g.remote_dma_fused([write(core, [near[c] for c, _ in TELL], spare, T.sem.hn, [T.hn[:, 0:2]] * len(TELL), T[nl][:, OWN:OWN + 2], topo, total)], local_sem=T.sem["ls"])
        arrive("adl%d" % t, len(off) * (N - 1), (nl,))
        for b in range(4):
            scan("lf" + n, "rst", "dt" + n, c0=(0, 32), c1=(0, 32), po=(0, 32), pi=quad[b], co=(32 * b, 32 * b + 32), a=("lf" + n,))
        for b in quad:
            ts("ko" + n, "lf" + n, 4.0, OP.mult, T.t4[0:32, 0:1], OP.add, r=("t4",), po=b, pi=(0, 32), ci=(3, 128, 4), a=("ko" + n,))
        for i in (0, 1):
            e = i ^ upper
            lo, c, made = 256 + 256 * e, NEW + HALF * (2 * e - 1), (h + "n%d" % i,)
            run("v", lambda: V.tensor_tensor(T[hb][:, lo:lo + 256], T.kd[:, 0:2048].indirect(ap("ko" + n, None, (16 * e, 16 * e + 16))), T[dq][:, 256 * e:256 * e + 256], OP.add),
                r=("kd", "ko" + n, dq), a=(hb + str(e),))
            quant(h, c + 128, hb, 512 * e, 512 * e + 512, c, (hb + str(e), hb + "z"), made)
            if i == 0:
                direct(leg, "c", h, 0, NEW, made, handed(leg, "s", h, NEW, slice(0, 1)))
            else:
                hand(leg, "s", h, NEW, slice(1, 3), made)
                direct(leg, "c", h, 1, NEW, made)
        for k in "cs":
            arrive("are%s%d" % (k, t), coming(leg, k), (h + k,))
        pick(h, HELD, HELD + A, "hq%d" % t, WIN if t else 0, HOME if t else 128, "lu" + n, None, (h + "n0",))

    q = quad[0]
    direct("x", "c", "hq0")
    hand("x", "c", "hq0")
    hand("x", "s", "hq0")
    both("la", A * me, A * me + A, "hq0", 0, A)
    ts("u_0", "stt", 256.0, OP.mult, T.af[q[0]:q[1], 0:1], OP.add, r=("af",), po=q, ci=(1, 2))
    unpack(0)
    route(0, q)
    iota("ia", [[1, 8], [0, 4]], 256, -1)
    iota("ic", [[1, 64]], 256, -1)
    cp("vl0", "pk0", co=(3, 4), ci=(0, 1), a=("vl0",))
    arrive("apk0", sum(len(l) for l in lanes(N - 1, len(off))), ("vl0",))
    arrive("aco0", coming("x"), ("lac", "las"))
    while later:
        gap()
    act("kp", "u_0", 1.0 / CAP, (HELD - WIN) / CAP, po=mine, pi=q, a=("kp",), r=("kp",))
    act("r2", "mask8", NEW + CAP * me - BACK - (N - 1) * CAP, "r1", ci=(0, 1))
    act("cloc", "cl1", 1, "r2")
    quant("kn", 512, "kb", 0, 2048)
    unpack(1)
    pick("kj", 0, 512, "kn", 0, 512, "ku")
    unpack_keys((0, 1))
    dma("y", [(T.nrow[0:1, :], T.nxt[0:32, 0:16])], r=("nxt",), w=("nrow",))
    run("g", lambda: g.partition_broadcast(T.tab[:], T.nrow[0:1, :], 128), r=("nrow",), w=("tab",))
    for b in (2, 3):
        unpack(b)
    unpack_keys((2, 3))
    ts("ia2", "ia", 3, OP.bitwise_and)
    ts("ic2", "ic", 15, OP.bitwise_and)
    cp("t4", "ip3")
    ts("mask", "ia2", 0.0, OP.is_equal, co=(0, 32), a=("mask",))
    ts("mask", "ic2", 0.0, OP.is_equal, co=(32, 96), a=("mask",))
    ts("lu_0", "iw", 16.0, OP.mult, T.r0[:, 0:1], OP.add, r=("r0",), ci=(0, 2))
    tt("vp_0", "vl0", "mask8", OP.mult, cx=(3, 11))
    ts("sr_0", "vl0", 255, OP.bitwise_and, ci=(3, 11))
    run("v", lambda: V.tensor_reduce(ap("pkf_0"), ap("vp_0"), X, OP.add), r=("vp_0",), w=("pkf_0",))
    cp("su_0", "sr_0", co=(me, N), ci=(0, N - me), a=("su_0",))
    cp("pki_0", "pkf_0")
    if me:
        cp("su_0", "sr_0", co=(0, me), ci=(N - me, N), a=("su_0",))
    leads = slots(0)
    mix(leads[:3])
    pick("ld0", 0, 128, "la", 0, N * A, "su_0")
    mix(leads[3:])
    both("fin", A, 128, "hq0", A, 128, ("lac", "las"))
    dma("y", [(T.wb[:], T.w[:, :])], w=("wb",))
    ahead(0)
    hop(0)
    cp("n_0", "stt", po=q, ci=(1, 2))
    act("maskp", "mask", PART, 0, ci=(32, 96))
    act("clp", "cloc", 1, RANK * me * (1 - PART))
    for t in range(1, R + 1):
        if t < R:
            route(t, mine)
            depart(t)
            mix(search(t), stand(t) + places(t))
            ahead(t)
            mix(slots(t))
            dma("y", [(T.nd[k:k + 1, 0:A], ap("n_%d" % k, mine if k else q)) for k in range(t if t > 1 else 0, t + 1)], r=("n_0", "n_%d" % t, "ld%dc" % t))
            hop(t)
        else:
            quant("wq", 128, "wb", 0, 512)
            rows(t, mine)
            mix(places(t), stand(t))
            dma("y", [(T.nd[t:t + 1, 0:A], ap("n_%d" % t, mine))], r=("n_%d" % t,))
            pick("fin", 0, A, "hq%d" % t, WIN, HOME, "lu_%d" % t)
            mm("z0", "wq", "fin", 0, 128)
            dma("y", [(T.oc[:, 0:4 * A], codes("fin", 0, A))], r=("finc",))
            dma("s", [(T.osc[4 * k:4 * k + 4, 0:A], T.fins[32 * k:32 * k + 4, 0:A]) for k in range(4)], r=("fins",))
            run("v", lambda: V.tensor_copy(T.yb[:], T.z0[:, 0:A]), r=("z0",), w=("yb",))
            dma("y", [(T.y[:, :], T.yb[:])], r=("yb",))
    for sem in total:
        if waited.get(sem, 0) < total[sem]:
            g.wait_ge(T.sem[sem], total[sem])
